import numpy as np, ml_dtypes
CORES = [10,34,74,98]
N = 4
BF = ml_dtypes.bfloat16
def gentries(a):
    return np.ascontiguousarray(a.reshape(8, 16, -1).transpose(0, 2, 1)).reshape(8, -1)
def gtable(e):
    e = np.asarray(e); return np.ascontiguousarray(e.reshape(8, -1, 16).transpose(0, 2, 1)).reshape(128, -1).astype(np.int32)
NL, H, L, K, S, RO = 4096, 2048, 64, 16, 1, 6
MT = [16, 12, 20, 14, 24, 10]
AT = [8, 10, 7, 9, 6, 11]
def own(rng, c):
    return np.take_along_axis(c, rng.integers(0, K, (N, 8, 1, L)), 2)[:, :, 0]
def parts(rng):
    v = rng.integers(0, 256, (N, 8, 16, NL))
    g = 2 * np.argsort(rng.random((N, 8, 16, H)), axis=-1) + rng.integers(0, 2, (N, 8, 16, H))
    c = rng.integers(0, NL, (N, 8, K, L)); d = rng.integers(0, NL, (N, 8, K, L))
    return v, g, c, d, own(rng, c)
def pack(v, g, c, d, l):
    return {"val": np.ascontiguousarray(v.reshape(N, 128, NL)).astype(np.float32).astype(BF), "gen": np.ascontiguousarray(g.reshape(N, 128, H)).astype(np.int32),
            "cla": np.stack([gtable(a.reshape(8, -1)) for a in c]), "par": np.stack([gtable(a.reshape(8, -1)) for a in d]), "lit": np.stack([gtable(a) for a in l])}
def setup_inputs(rng):
    return pack(*parts(rng))
def setup_inputs_corners(rng):
    v, g, c, d, l = parts(rng)
    top = rng.random((N, 8, 1, NL)) < 1.0 / K
    v = np.where(top, rng.choice(np.array([222, 223, 224, 240, 255]), v.shape), rng.choice(np.array([0, 1, 31, 32, 33, 100]), v.shape))
    v[0, 6] = 0; v[1, 6] = 255
    g[:, 0, 3] = 2 * np.arange(H); g[:, 0, 15] = 2 * np.arange(H) + 1
    g[:, 1] = g[:, 1, :1].copy(); g[:, 2, ::4] = 0; g[:, 2, 1::4] = NL - 1
    c[..., 0::5] = d[..., 0::5]
    c[..., 1::5] = c[:, :, :1, 1::5].copy()
    c[:, :, 1::2, 2::5] = c[:, :, 0::2, 2::5] ^ 1
    e = c[..., 3::5]; c[..., 3::5] = rng.choice(np.array([0, 1, NL - 2, NL - 1]), e.shape)
    l[..., 0::3] = 0; l[..., 1::3] = NL - 1; l[..., 2::3] = c[:, :, K - 1, 2::3]
    return pack(v, g, c, d, l)
def setup_inputs_crowd(rng):
    v, g, c, d, l = parts(rng)
    for q in range(N):
        for s in range(8):
            w = 2 * rng.permutation(H)[:2 * K] + rng.integers(0, 2, 2 * K); c[q, s] = w[:K, None]; d[q, s] = w[K:, None]
            j = 15 if s == 7 else int(rng.integers(0, 16)); k = K - 1 if s == 0 else int(rng.integers(0, K))
            im = g[q, s, j, w[:K] >> 1] ^ (w[:K] & 1); both = np.concatenate([im, im ^ 1])
            v[q, s][:, both] = np.minimum(v[q, s][:, both], 100); v[q, s][:, im[k]] = 255; l[q, s] = im[k]
            if s in (2, 5):
                turn = rng.random(L) < 0.5; c[q, s] = np.where(turn, c[q, s] ^ 1, c[q, s]); v[q, s][:, im[k] ^ 1] = 255
            if s & 1:
                o = 0 if s == 1 else L - 1 if s == 7 else int(rng.integers(0, L))
                c[q, s, :, o] = int(c[q, s, 0, o]); d[q, s, :, o] = int(d[q, s, 0, o])
    return pack(v, g, c, d, l)
def endclauses(rng):
    E = np.array([0, NL - 1]); sh = (N, 8, 1, L); b = rng.integers(0, 2, sh); x = E[b]; y = E[1 - b]; kind = rng.integers(0, 4, sh)
    k1 = rng.integers(0, K, sh); k2 = (k1 + rng.integers(1, K, sh)) % K; k = np.arange(K).reshape(1, 1, K, 1)
    c = np.where(k == k1, y, x); c = np.where((kind == 2) & (k == k2), x ^ 1, c)
    return np.where(kind == 3, E[rng.integers(0, 2, (N, 8, K, L))], c)
def setup_inputs_ends(rng):
    E = np.array([0, NL - 1]); v = 255 * rng.integers(0, 2, (N, 8, 16, NL)); g = E[rng.integers(0, 2, (N, 8, 16, H))]
    c = endclauses(rng); d = endclauses(rng); l = E[rng.integers(0, 2, (N, 8, L))]
    for o, k in ((0, 0), (L - 1, K - 1)):
        c[:, :, :, o] = NL - 1; c[:, :, k, o] = 0
    h = (np.arange(16) < 8).astype(np.int64); on = np.ones(16, np.int64); no = 0 * on
    for q in range(N):
        for s in range(8):
            ty = (3 * q + s) % 6
            if q == N - 1 and s == 7: ty = 0
            if q in (0, 2) and s == 6: ty = 6
            four = [[on, no, no, on], [no, on, on, no], [h, no, no, 1 - h], [no, h, 1 - h, no], list(rng.integers(0, 2, (4, 16))), [on, no, no, on], [on, no, no, no]][ty]
            four = np.stack(four)
            if ty == 5: four[:, 13:] = rng.integers(0, 2, (4, 3))
            if ty == 6: g[q, s, :2, 0] = NL - 1; g[q, s, 2:, 0] = 0
            v[q, s][:, [0, 1, NL - 2, NL - 1]] = 255 * four.T
    return pack(v, g, c, d, l)
def setup_inputs_spread(rng):
    v, g, c, d, l = parts(rng)
    v = np.minimum((1.1 * np.exp2(8 * rng.random((N, 8, 1, NL))) * rng.random((N, 8, 16, NL))).astype(np.int64), 255)
    v[:, 1::2] = np.minimum((256 * rng.random((N, 4, 16, NL)) ** np.exp2(rng.integers(-1, 3, (N, 4, 16, 1)))).astype(np.int64), 255)
    g[:, :, ::2] = 2 * np.minimum((H * rng.random((N, 8, 8, H)) ** 3).astype(np.int64), H - 1) + rng.integers(0, 2, (N, 8, 8, H))
    p = rng.choice(np.array([1, 2, 4]), (N, 8, 1, 1))
    c = np.minimum((NL * rng.random((N, 8, K, L)) ** p).astype(np.int64), NL - 1); d = NL - 1 - np.minimum((NL * rng.random((N, 8, K, L)) ** p).astype(np.int64), NL - 1)
    l = np.where(rng.random((N, 8, L)) < 0.5, own(rng, c), own(rng, d))
    return pack(v, g, c, d, l)
def apart(rng, v, g, c, d, l, s, one):
    w = rng.permutation(H); z = 2 * w[:L] + rng.integers(0, 2, L); r = w[L:]; m = np.zeros(H, np.int64)
    m[z >> 1] = np.roll(z, -1) ^ (z & 1); m[r] = 2 * rng.permutation(r) + rng.integers(0, 2, H - L); g[:, s, 0] = m
    v[:, s] = np.minimum(v[:, s], 100); v[:, s][:, :, z] = 255; v[:, s][:, :, z ^ 1] = rng.integers(200, 256, (N, 16, L))
    c[:, s] = 2 * r[rng.integers(0, H - L, (N, K, L))] + rng.integers(0, 2, (N, K, L))
    for q in range(N):
        y = rng.permutation(z); c[q, s, rng.integers(0, K, L), np.arange(L)] = y; l[q, s] = y
        if one:
            o = L - 1 if q == N - 1 else int(rng.integers(0, L))
            c[q, s, :, o] = int(c[q, s, 0, o]); d[q, s, :, o] = int(d[q, s, 0, o])
def setup_inputs_ties(rng):
    v, g, c, d, l = parts(rng); m = np.array(MT)[np.arange(8) % RO].reshape(1, 8, 1, 1); u = K * rng.random((N, 8, 1, NL))
    low = (rng.random(v.shape) * (255 - m)).astype(np.int64)
    w = np.where(u < 1, 255, np.where(u < 1.3, 255 - m, np.where(u < 4, 254 - m, low)))
    v = np.where(rng.random(v.shape) < 0.02, v, w)
    h = (np.arange(16) < 8).astype(np.int64).reshape(16, 1); x = u[:, [2, 5]]
    v[:, [2, 5]] = np.where(x < 1, 255 * h, np.where(x < 2, 255 * (1 - h), np.minimum(low[:, [2, 5]], 100)))
    eq = rng.random((N, 8, 1, H)) < 0.25; v[..., 1::2] = np.where(eq, v[..., 0::2], v[..., 1::2])
    apart(rng, v, g, c, d, l, 6, False); apart(rng, v, g, c, d, l, 7, True)
    return pack(v, g, c, d, l)
def check_inputs(d):
    bad = []
    for k, lo, hi in (("val", 0, 255), ("gen", 0, NL - 1), ("cla", 0, NL - 1), ("par", 0, NL - 1), ("lit", 0, NL - 1)):
        a = np.asarray(d[k]).astype(np.float64)
        if not (np.min(a) >= lo and np.max(a) <= hi): bad.append("range of " + k)
        elif np.any(a != np.floor(a)): bad.append("whole numbers of " + k)
    return bad
def reference(val, gen, cla, par, lit):
    V = val.astype(np.float32).astype(np.int16).reshape(N, 8, 16, NL)
    e = gen.astype(np.int64).reshape(N, 8, 16, H); P = np.stack([e, e ^ 1], axis=-1).reshape(N, 8, 16, NL)
    C = np.stack([gentries(a) for a in cla]).astype(np.int64).reshape(N, 8, K, L); D = np.stack([gentries(a) for a in par]).astype(np.int64).reshape(N, 8, K, L)
    l = np.stack([gentries(a) for a in lit]).astype(np.int64); A = np.zeros((N, 8), np.int64)
    for t in range(RO):
        if t: C = np.roll(C, S, axis=0); D = np.roll(D, S, axis=0); l = np.roll(l, S, axis=0)
        for a in range(N):
            v = V[a]; x = l[a][:, None, :]
            less = np.take_along_axis(v, x, 2) < np.take_along_axis(v, x ^ 1, 2)
            c = np.where((np.add.reduce(less.astype(np.int64), axis=1) >= 9)[:, None, :], D[a], C[a])
            img = np.take_along_axis(P[a], c.reshape(8, 1, K * L), 2)
            w = np.take_along_axis(v, img.reshape(8, 1, 16 * K * L), 2).reshape(8, 16, 16, K, L)
            near = w >= np.max(w, axis=3)[:, :, :, None] - MT[t]
            unit = np.add.reduce(near, axis=3, dtype=np.int16) == 1
            votes = np.add.reduce(unit.astype(np.int64), axis=1); js = np.argmax(votes, axis=1)
            pro = np.max(votes, axis=1) >= (AT[t] + (A[a] & 1))[:, None]
            new = np.take_along_axis(img.reshape(8, 16, K, L), js[:, None, None, :], 1)[:, 0]
            un = np.take_along_axis(unit, js[:, None, None, :], 2)[:, :, 0]
            vn = np.take_along_axis(v, new.reshape(8, 1, K * L), 2).reshape(8, 16, K, L).astype(np.int64)
            ks = np.argmax(np.add.reduce(np.where(un[:, :, None, :], vn, 0), axis=1), axis=1)
            nl = np.take_along_axis(new, ks[:, None, :], 1)[:, 0]
            C[a] = np.where(pro[:, None, :], new, D[a]); D[a] = c; l[a] = np.where(pro, nl, l[a])
            for g in range(8):
                z = nl[g, np.flatnonzero(pro[g])]
                z = z[np.unique(z >> 1, return_index=True)[1]]
                up = np.minimum(v[g][:, z] + 32, 255); down = np.maximum(v[g][:, z ^ 1] - 32, 0)
                v[g][:, z] = up; v[g][:, z ^ 1] = down
            A[a] = np.add.reduce(pro.astype(np.int64), axis=1)
    return {"yv": V.reshape(N, 128, NL).astype(np.float32).astype(BF), "yc": np.stack([gtable(a.reshape(8, -1)) for a in C]).astype(np.float32),
            "yd": np.stack([gtable(a.reshape(8, -1)) for a in D]).astype(np.float32), "yl": np.stack([gtable(a) for a in l]).astype(np.float32)}

@@ -1,0 +1,539 @@
+from concourse.mybir import AluOpType as A, AxisListType, ActivationFunctionType as F
+
+RO = 6
+MT = [16, 12, 20, 14, 24, 10]
+AT = [8, 10, 7, 9, 6, 11]
+PAD = 128
+NV = PAD + 4096
+OFF = PAD - 0.5
+M2, M4, M16K = 1.5 * 2 ** 24, 1.5 * 2 ** 25, 1.5 * 2 ** 37
+BIG = 1.0e9
+CHUNKS = [2, 2, 4, 4, 4, 4, 4, 4, 2, 2]
+PIECE = 2
+SHORT = 1
+IMG = [8]
+VSHARE = {}
+UNIT_ACT = 8
+PB = "aaaaqqqq"
+LOOK, BULK = 0.0, 20000.0
+
+f32, b16, i32, u16 = "float32", "bfloat16", "int32", "uint16"
+SCRATCH = {}
+for _n, _w, _d in (("IW", 160, f32), ("cA", 160, f32), ("c16", 128, f32), ("c32", 128, f32), ("cl", 64, f32), ("ri", 6, i32), ("cf", 16, f32),
+                   ("Ib", 128, b16), ("nI", 128, f32), ("I2", 128, f32), ("nIb", 128, b16), ("B", 144, b16), ("Z0", 128, b16), ("Z1", 128, b16), ("zc", 64, b16), ("O32", 128, f32), ("A00", 128, f32), ("A01", 128, f32),
+                   ("A10", 128, f32), ("A11", 128, f32), ("H0", 128, f32), ("H1", 128, f32), ("m32", 32, f32), ("EM", 130, b16), ("DM", 8, b16),
+                   ("K4", 4, f32), ("TC", 14, f32), ("CV", 32, b16), ("CK", 32, b16), ("msk", 2048, b16), ("rv", 32, f32),
+                   ("dl", 128, b16), ("ci", 132, i32), ("cfl", 132, f32), ("y1", 2048, f32), ("s", 8192, b16), ("finA", 132, f32), ("fin", 132, f32)):
+    SCRATCH[_n] = ("sbuf", [128, _w], _d)
+SCRATCH["Pb"] = ("sbuf", [128, 8208], b16)
+SCRATCH["E"] = ("sbuf", [128, 2048], b16)
+SCRATCH["Mx"] = ("sbuf", [128, 512], b16)
+for _f in (0, 1):
+    for _n, _w, _d in (("P", 4096, f32), ("V", NV, b16), ("gi", 2048, i32), ("w", 8192, b16), ("W", 584 * RO, f32), ("SB", 72 * RO, f32), ("I", 512, f32),
+                       ("Ou", 512, u16), ("U", 544, b16), ("unx", 512, b16), ("unb", 512, b16), ("pr", 512, b16), ("Lu", 4, u16),
+                       ("g1", 64, b16), ("less", 32, b16), ("Lc", 32, u16), ("ev", 32, f32), ("en", 4, i32),
+                       ("J", 2, u16), ("pro", 2, f32), ("sm", 2, f32), ("q", 32, f32), ("Cu", 32, u16), ("LT", 32, f32), ("L8", 32, f32), ("eq", 32, f32), ("mu", 32, f32),
+                       ("ex", 65, f32), ("d", 130, f32), ("T8", 8, u16), ("up", 128, b16), ("nw", 128, b16), ("X", 64, f32)):
+        SCRATCH[_n + str(_f)] = ("sbuf", [128, _w], _d)
+    for _b in range(4):
+        SCRATCH["ps%d%d" % (_f, _b)] = ("psum", [128, 512], f32)
+SEMAPHORES = ["eV", "eA", "eP", "eG", "sent", "ldc", "stv0", "stv1", "sto"] + ["ld%s%d" % (a, f) for a in "vg" for f in (0, 1)] \
+    + ["arr%s%d%d" % (a, t, f) for a in "ab" for t in range(1, RO) for f in (0, 1)]
+
+CY, GA, SCAT = 1.04, 1.56, 3.8
+LAT, NET = 160.0, 3000.0
+
+
+def build(T, dst_addr, emask, nen):
+    ops = []
+
+    def op(eng, fn, rd, wr, cost, bank=None, sem=None, inc=1):
+        ops.append({"e": eng, "fn": fn, "rd": rd, "wr": wr, "c": cost, "bk": bank, "sem": sem, "inc": inc})
+
+    def V(fn, rd, wr, n=64, bank=None):
+        op("V", fn, rd, wr, max(n, 64) * CY + 15, bank)
+
+    def ts(out, a, s1, s2, o0, o1, rd, wr, n=64, bank=None):
+        if o1 is None:
+            V(lambda e: e.tensor_scalar(out, a, s1, None, o0), rd, wr, n, bank)
+        else:
+            V(lambda e: e.tensor_scalar(out, a, s1, s2, o0, o1), rd, wr, n, bank)
+
+    def tt(out, a, b, o, rd, wr, n=64, bank=None):
+        V(lambda e: e.tensor_tensor(out, a, b, o), rd, wr, n, bank)
+
+    def cp(out, a, rd, wr, n=64, bank=None):
+        V(lambda e: e.tensor_copy(out, a), rd, wr, n, bank)
+
+    def ms(out, c, wr, n=64):
+        V(lambda e: e.memset(out, c), [], wr, n)
+
+    def scan(out, d0, d1, o0, o1, rd, wr, n=64, bank=None):
+        V(lambda e: e.tensor_tensor_scan(out, d0, d1, 0.0, o0, o1), rd, wr, n, bank)
+
+    def red(out, a, o, rd, wr, ab=False):
+        V(lambda e: e.tensor_reduce(out, a, AxisListType.X, o, apply_absolute_value=ab), rd, wr)
+
+    def tr(out, a, rd, wr, n=64, bank=None):
+        V(lambda e: e.transpose(out, a), rd, wr, n, bank)
+
+    def mm(out, l, r, st, sp, rd, bank, n=64, wide=False):
+        op("P", lambda e: e.matmul(out, l, r, st, sp), rd, [], max(n, 64) * (4 if wide else 1) * CY * 0.7, bank)
+
+    def act(out, a, rd, wr, n, bias=0.0, scale=1.0, bank=None, func=F.Identity):
+        op("A", lambda e: e.activation(out, a, func, bias=bias, scale=scale), rd, wr, n * CY + 65, bank)
+
+    def gat(out, a, rd, wr, n):
+        op("A", lambda e: e.activation(out, a, F.Copy), rd, wr, n * GA * CY + 65)
+        ops[-1]["g"] = 1
+
+    def io(out, pat, base, cm, wr, n, flag=True):
+        if flag:
+            op("G", lambda e: e.iota(out, pat, base, cm, allow_small_or_imprecise_dtypes=True), [], wr, 130 + 2 * n * CY)
+        else:
+            op("G", lambda e: e.iota(out, pat, base, cm), [], wr, 130 + 2 * n * CY)
+
+    def move(out, a, n, rd, wr):
+        op("G", lambda e: e.affine_select(out, a, [[0, n]], A.is_ge, 0.0, 0, 0), rd, wr, 170 + 2 * n * CY)
+
+    def dma(q, out, a, rd, wr, sem, lat):
+        op(q, lambda e: e.dma_start(out, a), rd, wr, 100, "dma" + q, sem, 16)
+        ops[-1]["lat"] = lat
+
+    dma("S", T.ci[:, 0:64], T.par[:], [], ["ci0"], "ldc", 2200)
+    dma("S", T.ci[:, 64:128], T.cla[:], [], ["ci1"], "ldc", 2200)
+    dma("S", T.ci[:, 128:132], T.lit[:], [], ["ci2"], "ldc", 2200)
+    for f in (0, 1):
+        for nm, src, buf, c0 in (("g", T.gen, T["gi%d" % f], 0), ("v", T.val, T["V%d" % f], PAD)):
+            for j in range(8):
+                gr = 2 * (j // 2) + f
+                dma("A" if f == 0 and j % 2 else "S", buf[16 * j:16 * j + 16, c0:], src[16 * gr:16 * gr + 16, :],
+                    ["ldv0%d" % z for z in range(8)] if f else [], ["ld%s%d%d" % (nm, f, j)],
+                    "ld%s%d" % (nm, f), 2500 + 2500 * (nm == "v") + 300 * j)
+    io(T.ri[:, 0:1], [[0, 1]], 0, 1, ["ri"], 1, False)
+    io(T.cA[:], [[1, 160]], -16, 0, ["cA"], 160)
+    io(T.c16[:], [[16, 8], [0, 16]], 0, 0, ["c16"], 128)
+    io(T.c32[:], [[32, 4], [0, 32]], 0, 0, ["c32"], 128)
+    io(T.cl[:], [[16, 2], [32, 2], [1, 16]], 0, 0, ["cl"], 64)
+    io(T.CK[:], [[-1, 16], [0, 2]], 15, 0, ["CK"], 32)
+    for j, m in enumerate((15, 16, 112, 96, 31)):
+        ts(T.ri[:, j + 1:j + 2], T.ri[:, 0:1], m, None, A.bitwise_and, None, ["ri"], ["ri%d" % j])
+    cf = T.cf
+    cp(cf[:, 0:6], T.ri[:], ["ri"] + ["ri%d" % j for j in range(5)], ["cf"])
+    cr, cp_, ch, c16r, c32r, c31 = [cf[:, j:j + 1] for j in range(6)]
+    ts(cf[:, 6:7], ch, 1.0 / 16, None, A.mult, None, ["cf"], ["h1"])
+    ts(cf[:, 7:8], ch, -1.0 / 16, 1.0, A.mult, A.add, ["cf"], ["h0"])
+    ts(cf[:, 8:9], ch, 2.0, cp_, A.mult, A.add, ["cf"], ["own0"])
+    ts(cf[:, 9:10], cf[:, 8:9], 16.0, None, A.add, None, ["own0"], ["own1"])
+    ts(cf[:, 10:11], ch, 4.0, cp_, A.mult, A.add, ["cf"], ["dm0"])
+    ts(cf[:, 11:12], cp_, -32.0, 1008.0, A.mult, A.add, ["cf"], ["cv0"])
+    ts(T.IW[:], T.cA[:], cr, None, A.is_equal, None, ["cA", "cf"], ["IW"], 160)
+    half = (cf[:, 7:8], cf[:, 6:7])
+    for x in (0, 1):
+        for y in (0, 1):
+            o = 16 - 16 * (y - x)
+            ts(T["A%d%d" % (x, y)][:], T.IW[:, o:o + 128], half[x], None, A.mult, None, ["IW", "h0", "h1"], ["A%d%d" % (x, y)], 128)
+        tt(T["H%d" % x][:], T["A%d0" % x][:], T["A%d1" % x][:], A.add, ["A%d0" % x, "A%d1" % x], ["H%d" % x], 256)
+    cp(T.Ib[:], T.IW[:, 16:144], ["IW"], ["Ib"], 128)
+    ts(T.nIb[:], T.IW[:, 16:144], -1.0, None, A.mult, None, ["IW"], ["nIb"], 128)
+    ts(T.nI[:], T.IW[:, 16:144], -1.0, None, A.mult, None, ["IW"], ["nI"], 128)
+    ts(T.I2[:], T.IW[:, 16:144], 2.0, None, A.mult, None, ["IW"], ["I2"], 128)
+    ts(T.Z0[:], T.c16[:], c16r, 16384.0, A.is_equal, A.mult, ["c16", "cf"], ["Z0"], 128)
+    ts(T.Z1[:], T.c16[:], c16r, -16384.0, A.is_equal, A.mult, ["c16", "cf"], ["Z1"], 128)
+    ms(T.zc[:], -8.5 * 16384, ["zc"]); ms(T.zc[:, 32:64], 8.5 * 16384, ["zc"])
+    ts(T.O32[:], T.c32[:], c32r, None, A.is_equal, None, ["c32", "cf"], ["O32"], 128)
+    ms(T.B[:], 0.0, ["B"])
+    ts(T.B[:, 16:144:16], T.c16[:, 0:128:16], c16r, 1024.0, A.is_equal, A.mult, ["c16", "cf"], ["B"])
+    ts(T.m32[:], T.cA[:, 16:48], c31, None, A.is_equal, None, ["cA", "cf"], ["m32"])
+    ms(T.EM[:], 0.0, ["EM"])
+    for q in (0, 1):
+        ts(T.EM[:, 65 * q:65 * q + 64], T.cl[:], cf[:, 8 + q:9 + q], 2.0 ** 28, A.is_ge, A.mult, ["cl", "own0", "own1", "EM"], ["EM%d" % q])
+    ts(T.DM[:], T.c16[:, 0:128:16], cp_, None, A.add, None, ["c16", "cf"], ["DM"])
+    ts(cf[:, 12:16], T.c16[:, 0:64:16], cf[:, 10:11], -1.0, A.add, A.mult, ["c16", "dm0"], ["k40"])
+    ts(T.K4[:], cf[:, 12:16], 4096.5, None, A.add, None, ["k40"], ["K4"])
+    ts(T.CV[:], T.c16[:, 0:32], -1.0, cf[:, 11:12], A.mult, A.add, ["c16", "cv0"], ["CV"])
+    ts(T.TC[:, 12:14], T.c16[:, 0:32:16], cp_, -8.0, A.add, A.mult, ["c16", "cf"], ["TCb"])
+    for t in range(RO):
+        ts(T.TC[:, 2 * t:2 * t + 2], T.TC[:, 12:14], 8.0 * (1024 * AT[t] + 511), None, A.add, None, ["TCb"], ["TC%d" % t])
+    ms(T.rv[:], 1.0, ["rv"]); ms(T.rv[:, 0:32:16], -BIG, ["rv"])
+    nm_ = max(512, PIECE * 256)
+    ms(T.msk[:, 0:nm_], 1.0, ["msk"], nm_ // 2); ms(T.msk[:, 0:nm_:16], 0.0, ["msk"])
+    ms(T.dl[:], 32.0, ["dl"]); ms(T.dl[:, 32:64], -32.0, ["dl"]); ms(T.dl[:, 96:128], -32.0, ["dl"])
+    ms(T.Pb[:, 0:1], 0.0, ["Pb0"])
+    ts(T.cfl[:], T.ci[:], OFF, None, A.add, None, ["ci0", "ci1", "ci2"], ["cfl"], 132)
+    AK = ["A00", "A01", "A10", "A11"]
+
+    def phase_setup(f):
+        B = lambda n: T[n + str(f)]
+        k = lambda n: n + str(f)
+        ps = [T["ps%d%d" % (f, b)] for b in range(4)]
+        bk = ["bk%d%d" % (f, b) for b in range(4)]
+        W = B("W")
+        ms(B("V")[:, 0:PAD], 0.0, [k("V")])
+        ms(B("U")[:, 512:544], 0.0, [k("Up")])
+        ms(B("unx")[:], 0.0, [k("unx")], 256)
+        ms(B("ex")[:, 64:65], 0.0, [k("exp")])
+        for j in (0, 1):
+            for h in (0, 1):
+                for q in (0, 1):
+                    mm(ps[2][:, 32 * j + 16 * h:32 * j + 16 * h + 16], T["A%d%d" % (f, q)][:], T.cfl[:, 64 * j + 2 * h + q:64 * j + 64:4], q == 0, q == 1,
+                       ["cfl"] + AK, bk[2], 16, True)
+        for h in (0, 1):
+            mm(ps[2][:, 64:66], T["A%d%d" % (f, h)][:], T.cfl[:, 128 + 2 * h:130 + 2 * h], h == 0, h == 1, ["cfl"] + AK, bk[2], 2, True)
+        tr(W[:, 512:576], ps[2][:, 0:64], [], [k("in0")], 64, bk[2])
+        cp(W[:, 576:578], ps[2][:, 64:66], [], [k("in0a")], 64, bk[2])
+        q_ = B("q")
+        ts(q_[:, 8:10], W[:, 576:578], M2, -M2, A.add, A.add, [k("in0a")], [k("r")])
+        tt(q_[:, 10:12], q_[:, 8:10], W[:, 576:578], A.subtract, [k("r"), k("in0a")], [k("r1")])
+        tt(W[:, 578:580], q_[:, 10:12], q_[:, 8:10], A.add, [k("r"), k("r1")], [k("in0b")])
+        ts(q_[:, 0:2], T.TC[:, 0:2], 0.125, None, A.mult, None, ["TC0"], [k("T")])
+        gl = ["ldg%d%d" % (f, j) for j in range(8)]
+        P = B("P")
+        first = len(ops)
+        for i in range(4):
+            ev, od = P[:, 1024 * i:1024 * i + 1024:2], P[:, 1024 * i + 1:1024 * i + 1024:2]
+            y = T.y1[:, 512 * i:512 * i + 512]
+            b = 3 * (i % 2)
+            ts(ev, B("gi")[:, 512 * i:512 * i + 512], OFF, None, A.add, None, gl, [k("Pe%d" % i)], 512)
+            how = PB[4 * f + i]
+            if how == "a":
+                act(y, ev, [k("Pe%d" % i)], ["y%d" % i], 512, M4, 2.0)
+                act(ps[b][:], y, ["y%d" % i], [], 512, -M4, 1.0, bk[b])
+                tt(od, ps[b][:], ev, A.subtract, [k("Pe%d" % i)], [k("Po%d" % i)], 512, bk[b])
+            elif how == "v":
+                ts(y, ev, 2.0, M4, A.mult, A.add, [k("Pe%d" % i)], ["y%d" % i], 512)
+                ts(ps[b][:], y, -M4, None, A.add, None, ["y%d" % i], [k("z%d" % b)], 512, bk[b])
+                tt(od, ps[b][:], ev, A.subtract, [k("Pe%d" % i), k("z%d" % b)], [k("Po%d" % i)], 512, bk[b])
+            else:
+                ts(y, ev, M2, -M2, A.add, A.add, [k("Pe%d" % i)], ["y%d" % i], 512)
+                mm(ps[b][:], T.I2[:], y, True, False, ["I2", "y%d" % i], bk[b], 512, True)
+                mm(ps[b][:], T.nI[:], ev, False, True, ["nI", k("Pe%d" % i)], bk[b], 512, True)
+                if how == "p":
+                    act(od, ps[b][:], [], [k("Po%d" % i)], 512, 0.0, 1.0, bk[b])
+                else:
+                    cp(od, ps[b][:], [], [k("Po%d" % i)], 512, bk[b])
+        for o in ops[first:]:
+            o["bulk"] = f
+
+    def phase(t, f):
+        B = lambda n: T[n + str(f)]
+        k = lambda n: n + str(f)
+        ps = [T["ps%d%d" % (f, b)] for b in range(4)]
+        bk = ["bk%d%d" % (f, b) for b in range(4)]
+        w0, s0 = 584 * t, 72 * t
+        W, SB, q_ = B("W"), B("SB"), B("q")
+        Wc = lambda a, b, c=1: W[:, w0 + a:w0 + b:c] if c > 1 else W[:, w0 + a:w0 + b]
+        Sc = lambda a, b: SB[:, s0 + a:s0 + b]
+        INL = [k("in0a"), k("in0b")] if t == 0 else [k("inb%d_" % t)]
+        IN = INL + [k("in0") if t == 0 else k("ina%d_" % t)]
+        VK = [k("V")] + (["ldv%d%d" % (f, j) for j in range(8)] if t == 0 else [])
+        PK = [k("P%s%d" % (a, i)) for a in "eo" for i in range(4)]
+        Vw = B("V")[:, 0:NV]
+        sb = lambda n: "%s%d%d" % (n, t, f)
+
+        def send(part, a, b, rd):
+            if t + 1 < RO:
+                sem = "arr%s%d%d" % (part, t + 1, f)
+                op("G", lambda e: e.remote_dma(W[:, w0 + 584 + 512 + a:w0 + 584 + 512 + b], Sc(a, b), T.sem[sem], T.sem.sent, dst_addr[1], dst_addr[0], emask),
+                   rd, [sb("gone" + part)], 300, None, "sent", 0)
+                op("N", None, [sb("gone" + part)], [k("in%s%d_" % (part, t + 1))], NET, None, sem, nen)
+
+        ts(B("Lu")[:], Wc(576, 580), 0.5, None, A.add, None, INL, [k("Lu")])
+        cp(B("g1")[:], Vw.indirect(B("Lu")[:, 0:4]), VK + [k("Lu")], [k("g1")], 50 + 64 * GA)
+        tt(B("less")[:], B("g1")[:, 0:32], B("g1")[:, 32:64], A.is_lt, [k("g1")], [k("less")])
+        for x in (0, 1):
+            o = ps[2][:, 300 + 32 * x:332 + 32 * x]
+            mm(o, T.Ib[:], T.zc[:, 32 * x:32 * x + 32], True, False, ["Ib", "zc"], bk[2])
+            mm(o, T["Z%d" % x][:], B("less")[:], False, True, ["Z0", "Z1", k("less")], bk[2])
+        tt(B("X")[:], ps[2][:, 300:364], Wc(512, 576), A.min, IN, [k("XX")], 64, bk[2])
+        tt(Sc(0, 32), B("X")[:, 0:32], B("X")[:, 32:64], A.max, [k("XX")], [sb("c")])
+        for x in (0, 1):
+            for y in (0, 1):
+                mm(ps[2][:, 32 + x:64:2], T["A%d%d" % (x, y)][:], Sc(16 * y, 16 * y + 16), y == 0, y == 1, [sb("c")] + AK, bk[2], 16, True)
+        ts(B("Lc")[:], ps[2][:, 32:64], -OFF, None, A.add, None, [], [k("Lc")], 64, bk[2])
+        for u, (a, b) in enumerate(zip([0] + IMG, IMG + [32])):
+            gat(B("I")[:, 16 * a:16 * b], B("P")[:, 0:4096].indirect(B("Lc")[:, a:b]), PK + [k("Lc")], [k("I%d" % u)], 16 * (b - a))
+            tr(Wc(16 * a, 16 * b), B("I")[:, 16 * a:16 * b], [k("I%d" % u)], [sb("O%d" % u)], 16 * (b - a))
+            ts(B("Ou")[:, 16 * a:16 * b], Wc(16 * a, 16 * b), 0.5, None, A.add, None, [sb("O%d" % u)], [k("Ou_%d_" % z) for z in range(a, b)], 16 * (b - a))
+        a0 = 0
+        UK = []
+        for ci, n in enumerate(CHUNKS):
+            nv = VSHARE.get((t, f, ci), 0)
+            lk = lambda nm, a, b: [k("%s_%d_" % (nm, x)) for x in range(a, b)]
+            ou = lk("Ou", a0, a0 + n)
+            gat(B("w")[:, 256 * a0:256 * (a0 + n - nv)], Vw.indirect(B("Ou")[:, 16 * a0:16 * (a0 + n - nv)]), VK + ou, lk("w", a0, a0 + n - nv), 256 * (n - nv))
+            ops[-1]["bulk"] = 1
+            ops[-1]["bk"] = "gathers"
+            if nv:
+                cp(B("w")[:, 256 * (a0 + n - nv):256 * (a0 + n)], Vw.indirect(B("Ou")[:, 16 * (a0 + n - nv):16 * (a0 + n)]), VK + ou, lk("w", a0 + n - nv, a0 + n), 50 + 256 * nv * GA)
+            mx = T.Mx[:, 16 * a0:16 * (a0 + n)]
+            mk_ = ["Mx_%d" % z for z in range(a0, a0 + n)]
+            short = ci >= len(CHUNKS) - SHORT
+            for a in range(a0, a0 + n, PIECE):
+                b = min(a + PIECE, a0 + n)
+                ne = 128 * (b - a)
+                if short:
+                    e0 = 256 * (a - 32 + sum(CHUNKS[-SHORT:]))
+                    e1 = e0 + 256 * (b - a)
+                    ek = ["E_%d" % z for z in range(a, b)]
+                    scan(T.E[:, e0:e1], B("w")[:, 256 * a - 1:256 * b - 1], T.msk[:, 0:256 * (b - a)], A.max, A.mult, lk("w", a - 1, b) + ["msk"], ek, ne)
+                    ops[-1]["bulk"] = 1
+                    scan(T.s[:, 256 * a:256 * b], B("w")[:, 256 * a:256 * b], T.E[:, e0:e1], A.max, A.min, lk("w", a, b) + ek, ["s_%d" % z for z in range(a, b)], ne)
+                    ops[-1]["bulk"] = 1
+                    if b == a0 + n:
+                        tt(mx, T.E[:, e1 - 256 * n + 15:e1:16], B("w")[:, 256 * a0 + 15:256 * b:16], A.max, lk("w", a0, b) + ["E_%d" % z for z in range(a0, b)], mk_, 32 * n)
+                else:
+                    scan(T.Pb[:, 256 * a + 1:256 * b + 1], T.msk[:, 0:256 * (b - a)], B("w")[:, 256 * a:256 * b], A.mult, A.max, lk("w", a, b) + ["msk"],
+                         ["Pb_%d" % z for z in range(a, b)], ne)
+                    ops[-1]["bulk"] = 1
+            if not short:
+                tops = T.Pb[:, 256 * a0 + 16:256 * (a0 + n) + 1:16]
+                pk = ["Pb_%d" % z for z in range(a0, a0 + n)]
+                move(mx, tops, 16 * n, pk, mk_)
+                io(tops, [[0, 16 * n]], 0, 0, pk, 16 * n)
+                for a in range(a0, a0 + n, PIECE):
+                    b = min(a + PIECE, a0 + n)
+                    scan(T.s[:, 256 * a:256 * b], B("w")[:, 256 * a:256 * b], T.Pb[:, 256 * a:256 * b], A.max, A.min,
+                         lk("w", a, b) + ["Pb_%d" % z for z in range(max(a - 1, 0), b)] + ["Pb0"], ["s_%d" % z for z in range(a, b)], 128 * (b - a))
+                    ops[-1]["bulk"] = 1
+            db = 3 * ((len(CHUNKS) - 1 - ci) % 2)
+            dps = ps[db][:, 16 * a0:16 * (a0 + n)]
+            mm(dps, T.Ib[:], T.Mx[:, 16 * a0:16 * (a0 + n)], True, False, ["Mx_%d" % z for z in range(a0, a0 + n)] + ["Ib"], bk[db], 16 * n)
+            mm(dps, T.nIb[:], T.s[:, 256 * a0 + 15:256 * (a0 + n):16], False, True, ["s_%d" % z for z in range(a0, a0 + n)] + ["nIb"], bk[db], 16 * n)
+            uk = k("U%d" % ci)
+            UK.append(uk)
+            if ci < UNIT_ACT:
+                act(B("U")[:, 16 * a0:16 * (a0 + n)], dps, [], [uk], 16 * n, -256.0 * (MT[t] + 0.5), 256.0, bk[db], F.Sigmoid)
+            else:
+                ts(B("U")[:, 16 * a0:16 * (a0 + n)], dps, MT[t] + 0.5, None, A.is_gt, None, [], [uk], 16 * n, bk[db])
+            for p in range(a0 // 2, (a0 + n) // 2):
+                if p == 0:
+                    mm(ps[1][:, 0:32], T.Ib[:], T.CV[:], True, False, ["Ib", "CV"], bk[1])
+                mm(ps[1][:, 0:32], T.B[:, 16 - p:144 - p], B("U")[:, 32 * p:32 * p + 32], False, p == 15, ["B", uk], bk[1])
+            a0 += n
+        en = B("en")
+        scan(B("ev")[:], T.rv[:], ps[1][:, 0:32], A.add, A.max, ["rv"], [k("ev")], 64, bk[1])
+        tt(en[:, 0:2], B("ev")[:, 15:32:16], q_[:, 0:2], A.max, [k("ev"), k("T")], [k("en")])
+        ts(en[:, 2:4], en[:, 0:2], 1023, None, A.bitwise_and, None, [k("en")], [k("enx")])
+        ts(B("J")[:], en[:, 2:4], -1.0, 1023.0, A.mult, A.add, [k("enx")], [k("J")])
+        pro = B("pro")
+        ts(pro[:], en[:, 2:4], 511.5, 8192.0, A.is_ge, A.mult, [k("enx")], [k("pro")])
+        OK = [sb("O%d" % u) for u in range(len(IMG) + 1)] + [k("J")] + IN
+        ts(B("Cu")[:], Wc(0, 544).indirect(B("J")[:, 0:2]), 0.5, None, A.add, None, OK, [k("Cu")], 100)
+        cp(B("unx")[:, 0:512:16], B("U")[:, 0:544].indirect(B("J")[:, 0:2]), UK + [k("Up"), k("J")], [k("unx")], 100)
+        cp(Sc(32, 64), Wc(0, 544).indirect(B("J")[:, 0:2]), OK, [sb("C")], 100)
+        send("a", 0, 64, [sb("c"), sb("C")])
+        scan(B("unb")[:], T.msk[:, 0:512], B("unx")[:], A.mult, A.add, ["msk", k("unx")], [k("unb")], 256)
+        for h in (0, 1):
+            for q in (0, 1):
+                mm(ps[2][:, 64 + 16 * h:80 + 16 * h], T["A%d%d" % (h, q)][:], Sc(32 + 16 * q, 48 + 16 * q), q == 0, q == 1, [sb("C")] + AK, bk[2], 16, True)
+        tr(B("LT")[:], ps[2][:, 64:96], [], [k("LT")], 64, bk[2])
+        for q in (0, 1):
+            ts(B("L8")[:, 16 * q:16 * q + 16], B("LT")[:, 16 * q:16 * q + 16], Wc(576 + q, 577 + q), pro[:, q:q + 1], A.subtract, A.mult, [k("LT"), k("pro")] + IN, [k("L8%d" % q)])
+        for q in (0, 1):
+            tt(B("pr")[:, q:512:2], Vw.indirect(B("Cu")[:, 16 * q:16 * q + 16]), B("unb")[:, 256 * q:256 * q + 256], A.mult,
+               VK + [k("Cu"), k("unb")], [k("pr%d" % q)], 50 + 256 * GA)
+        mm(ps[1][:, 32:64], T.Ib[:], T.CK[:], True, False, ["Ib", "CK"], bk[1])
+        for p in range(16):
+            mm(ps[1][:, 32:64], T.B[:, 16 - p:144 - p], B("pr")[:, 32 * p:32 * p + 32], False, p == 15, ["B", k("pr0"), k("pr1")], bk[1])
+        for q in (0, 1):
+            V(lambda e, q=q: e.tensor_reduce(B("sm")[:, q:q + 1], ps[1][:, 32 + q:64:2], AxisListType.X, A.max), [], [k("sm%d" % q)], 64, bk[1])
+        for q in (0, 1):
+            ts(B("eq")[:, 16 * q:16 * q + 16], ps[1][:, 32 + q:64:2], B("sm")[:, q:q + 1], 1.0 / 8192, A.is_equal, A.mult, [k("sm%d" % q)], [k("eq%d" % q)], 64, bk[1])
+        tt(B("mu")[:], B("eq")[:], B("L8")[:], A.mult, [k("eq0"), k("eq1"), k("L80"), k("L81")], [k("mu")])
+        scan(B("eq")[:], T.msk[:, 0:32], B("mu")[:], A.mult, A.add, ["msk", k("mu")], [k("eq0"), k("eq1")])
+        tt(Sc(64, 66), B("eq")[:, 15:32:16], Wc(576, 578), A.add, [k("eq0"), k("eq1")] + IN, [sb("l")])
+        LK = [sb("l")]
+        ts(q_[:, 8:10], Sc(64, 66), M2, -M2, A.add, A.add, LK, [k("r")])
+        for q in (0, 1):
+            ts(B("ex")[:, 32 * q:32 * q + 32], T.m32[:], Sc(64 + q, 65 + q), pro[:, q:q + 1], A.mult, A.mult, ["m32", sb("l"), k("pro")], [k("ex%d" % q)])
+        tt(q_[:, 10:12], q_[:, 8:10], Sc(64, 66), A.subtract, [k("r")] + LK, [k("r1")])
+        tt(Sc(66, 68), q_[:, 10:12], q_[:, 8:10], A.add, [k("r"), k("r1")], [sb("lp")])
+        send("b", 64, 68, [sb("lp")] + LK)
+        tt(q_[:, 12:14], q_[:, 8:10], pro[:], A.mult, [k("r"), k("pro")], [k("ep")])
+        tt(q_[:, 16:20], Sc(64, 68), T.K4[:], A.add, LK + [sb("lp"), "K4"], [k("A2")])
+        for q in (0, 1):
+            o = ps[3][:, 65 * q:65 * q + 65]
+            mm(o, T.Ib[:], T.EM[:, 65 * q:65 * q + 65], True, False, ["Ib", "EM", "EM0", "EM1"], bk[3])
+            mm(o, T.O32[:], B("ex")[:], False, True, ["O32", k("ex0"), k("ex1"), k("exp")], bk[3], 65, True)
+        for q in (0, 1):
+            ts(B("d")[:, 65 * q:65 * q + 65], ps[3][:, 65 * q:65 * q + 65], q_[:, 12 + q:13 + q], None, A.subtract, None, [k("ep")], [k("d%d" % q)], 65, bk[3])
+        for q in (0, 1):
+            red(q_[:, 14 + q:15 + q], B("d")[:, 65 * q:65 * q + 65], A.min, [k("d%d" % q)], [k("mn%d" % q)], True)
+            ts(q_[:, 20 + q:24:2], q_[:, 16 + q:20:2], q_[:, 14 + q:15 + q], 4096.0, A.min, A.max, [k("mn%d" % q), k("A2")], [k("X%d" % q)])
+        for x in (0, 1):
+            o = ps[3][:, 136 + 4 * x:140 + 4 * x]
+            mm(o, T.Ib[:], T.DM[:, 4 * x:4 * x + 4], True, False, ["Ib", "DM"], bk[3])
+            mm(o, T["H%d" % x][:], q_[:, 20:24], False, True, ["H0", "H1", k("X0"), k("X1")], bk[3], 4, True)
+        ts(B("T8")[:], ps[3][:, 136:144], -4096.0, None, A.add, None, [], [k("T8")], 64, bk[3])
+        tt(B("up")[:], Vw.indirect(B("T8")[:, 0:8]), T.dl[:], A.add, VK + [k("T8"), "dl"], [k("up")], 50 + 128 * GA)
+        ts(B("nw")[:], B("up")[:], 0.0, 255.0, A.max, A.min, [k("up")], [k("nw")])
+        cp(Vw.indirect(B("T8")[:, 0:8]), B("nw")[:], VK[1:] + [k("nw"), k("T8")], [k("V")], 50 + 128 * SCAT)
+        if t + 1 < RO:
+            for q in (0, 1):
+                mm(ps[2][:, 96:97], T.O32[:], pro[:, q:q + 1], q == 0, q == 1, ["O32", k("pro")], bk[2], 1, True)
+            ts(q_[:, 24:25], ps[2][:, 96:97], -4096.0, M16K, A.add, A.add, [], [k("a1")], 64, bk[2])
+            ts(q_[:, 25:26], q_[:, 24:25], -M16K, ps[2][:, 96:97], A.add, A.subtract, [k("a1")], [k("a2")], 64, bk[2])
+            ts(q_[:, 0:2], T.TC[:, 2 * t + 2:2 * t + 4], q_[:, 25:26], 0.125, A.subtract, A.mult, ["TC%d" % (t + 1), k("a2")], [k("T")])
+        else:
+            tr(B("X")[:], Sc(0, 64), [sb("c"), sb("C")], [k("XX")])
+            for j in (0, 1):
+                for h in (0, 1):
+                    for q in (0, 1):
+                        mm(ps[2][:, 128 + 64 * j + 2 * h + q:192 + 64 * j:4], T["A%d%d" % (q, f)][:], B("X")[:, 32 * j + 16 * h:32 * j + 16 * h + 16], True, True,
+                           [k("XX")] + AK, bk[2], 16, True)
+            for h in (0, 1):
+                mm(ps[2][:, 256 + 2 * h:258 + 2 * h], T["A%d%d" % (h, f)][:], Sc(64, 66), True, True, LK + AK, bk[2], 2, True)
+            if f == 0:
+                ts(T.finA[:], ps[2][:, 128:260], -OFF, None, A.add, None, [], ["finA"], 132, bk[2])
+            else:
+                tt(T.fin[:], ps[2][:, 128:260], T.finA[:], A.add, ["finA"], ["fin"], 132, bk[2])
+                dma("S", T.yd[:], T.fin[:, 0:64], ["fin"], [], "sto", 2000)
+                dma("S", T.yc[:], T.fin[:, 64:128], ["fin"], [], "sto", 2000)
+                dma("S", T.yl[:], T.fin[:, 128:132], ["fin"], [], "sto", 2000)
+            for j in range(4):
+                r0 = 32 * j + 16 * f
+                dma("A" if f == 1 and j % 2 else "S", T.yv[r0:r0 + 16, :], B("V")[r0:r0 + 16, PAD:], [k("V")], [], "stv%d" % f, 3000)
+
+    phase_setup(0)
+    phase_setup(1)
+    for t in range(RO):
+        phase(t, 0)
+        phase(t, 1)
+    return ops
+
+
+def link(ops):
+    lw, rdrs = {}, {}
+    for i, o in enumerate(ops):
+        hard, soft = set(), set()
+        for key in o["rd"]:
+            hard.add(lw[key])
+        for key in o["wr"]:
+            if key in lw:
+                hard.add(lw[key])
+            hard.update(rdrs.get(key, []))
+        b = o["bk"]
+        if b is not None:
+            if b in lw:
+                (soft if ops[lw[b]]["e"] == o["e"] else hard).add(lw[b])
+            lw[b] = i
+        for key in o["rd"]:
+            rdrs.setdefault(key, []).append(i)
+        for key in o["wr"]:
+            lw[key] = i
+            rdrs[key] = []
+        hard.discard(i)
+        o["hard"], o["soft"] = hard, soft - hard
+
+
+def schedule(ops):
+    n = len(ops)
+    succ = [[] for _ in ops]
+    for i, o in enumerate(ops):
+        for j in o["hard"] | o["soft"]:
+            succ[j].append(i)
+    pri = [0.0] * n
+    for i in range(n - 1, -1, -1):
+        o = ops[i]
+        pri[i] = o["c"] + o.get("lat", 0) + max([pri[j] + (LAT if i in ops[j]["hard"] else 0) for j in succ[i]] + [0])
+    left = [len(o["hard"] | o["soft"]) for o in ops]
+    rdy = [0.0] * n
+    free = {e: 0.0 for e in "VAPGSN"}
+    cand = {e: [] for e in "VAPGSN"}
+    for i in range(n):
+        if left[i] == 0:
+            cand[ops[i]["e"]].append(i)
+    order = {e: [] for e in "VAPGSN"}
+    end = 0.0
+    busy = {e: 0.0 for e in "VAPGSN"}
+    for _ in range(n):
+        best = None
+        for e in cand:
+            if cand[e]:
+                t0 = max(free[e], min(rdy[i] for i in cand[e]))
+                if best is None or t0 < best[0]:
+                    best = (t0, e)
+        t0, e = best
+        i = max((i for i in cand[e] if rdy[i] <= t0), key=lambda i: pri[i] - BULK * ops[i].get("bulk", 0))
+        if ops[i].get("bulk"):
+            soon = [j for j in cand[e] if rdy[j] <= t0 + LOOK and not ops[j].get("bulk")]
+            if soon:
+                i = min(soon, key=lambda j: rdy[j])
+        t0 = max(t0, rdy[i])
+        cand[e].remove(i)
+        o = ops[i]
+        o["t0"] = t0
+        done = t0 + o["c"]
+        busy[e] += o["c"]
+        if e != "N":
+            free[e] = done
+        order[e].append(i)
+        fin = done + o.get("lat", 0)
+        end = max(end, fin)
+        for j in succ[i]:
+            rdy[j] = max(rdy[j], fin + LAT if i in ops[j]["hard"] else done)
+            left[j] -= 1
+            if left[j] == 0:
+                cand[ops[j]["e"]].append(j)
+    return order, end, busy
+
+
+def rank_program(g, core, T, topo):
+    rank = T.rank_of(core)
+    if rank is None:
+        return
+    nxt = T.cores[(rank + 1) % len(T.cores)]
+    eng = topo.engines(core, nxt)
+    ops = build(T, topo.addr(nxt), topo.mask(core, nxt), len(eng))
+    link(ops)
+    order, _, _ = schedule(ops)
+    queue = {"V": g.vector, "A": g.scalar, "P": g.tensor, "G": g, "S": g.sync}
+    total = {}
+    for o in ops:
+        if o["sem"]:
+            total[o["sem"]] = total.get(o["sem"], 0) + o["inc"]
+    total["sent"] = len(eng) * sum(1 for o in ops if o["sem"] == "sent")
+    for e in "VAPG":
+        c = 0
+        for i in order[e]:
+            if not ops[i]["sem"]:
+                c += 1
+                ops[i]["tick"] = ("e" + e, c)
+        total["e" + e] = c
+    for o in ops:
+        if o["sem"]:
+            o["tick"] = (o["sem"], total[o["sem"]])
+    know = {e: {} for e in "VAPGS"}
+    waits = {}
+    for i in sorted(range(len(ops)), key=lambda i: (ops[i]["t0"], i)):
+        o = ops[i]
+        if o["e"] == "N":
+            o["vc"] = {}
+            continue
+        kn = know[o["e"]]
+        need = {}
+        for j in o["hard"]:
+            s, v = ops[j]["tick"]
+            if kn.get(s, 0) < v and need.get(s, (0, 0))[0] < v:
+                need[s] = (v, j)
+        for s in list(need):
+            if any(ops[j]["vc"].get(s, 0) >= need[s][0] for s2, (v, j) in need.items() if s2 != s):
+                del need[s]
+        waits[i] = [(s, v) for s, (v, j) in need.items()]
+        for s, (v, j) in need.items():
+            kn[s] = max(kn.get(s, 0), v)
+            for s2, v2 in ops[j]["vc"].items():
+                kn[s2] = max(kn.get(s2, 0), v2)
+        o["vc"] = dict(kn)
+    for e in "SAGVP":
+        q = queue[e]
+        for i in order[e]:
+            o = ops[i]
+            for s, v in waits[i]:
+                q.wait_ge(T.sem[s], v)
+            ins = o["fn"](q)
+            if o["sem"] != "sent":
+                ins.then_inc(T.sem[o["tick"][0]], o["inc"])
+    for s in SEMAPHORES:
+        g.wait_ge(T.sem[s], total[s])

@@ -6,23 +6,28 @@ AT = [8, 10, 7, 9, 6, 11]
 PAD = 128
 NV = PAD + 4096
 OFF = PAD - 0.5
-M2, M4, M16K = 1.5 * 2 ** 24, 1.5 * 2 ** 25, 1.5 * 2 ** 37
+M2, M4, M2K = 1.5 * 2 ** 24, 1.5 * 2 ** 25, 1.5 * 2 ** 34
 BIG = 1.0e9
-CHUNKS = [2, 2, 4, 4, 4, 4, 4, 4, 2, 2]
+CHUNKS = [4, 4, 4, 4, 4, 4, 4, 2, 2]
 PIECE = 2
 SHORT = 1
 IMG = [8]
-VSHARE = {}
-UNIT_ACT = 8
+SUMS = []
+PEF = 0.5
+DEFER = 14
+NUDGE, SEED = 0.0, 0
+JOIN = (0, 1, 3, 4)
+VSHARE = {(RO - 1, 1, 4): 1, (RO - 1, 1, 5): 1, (RO - 1, 1, 6): 1}
+UNIT_ACT = 6
 PB = "aaaaqqqq"
-LOOK, BULK = 0.0, 20000.0
+LOOK, BULK = 40.0, 20000.0
 
 f32, b16, i32, u16 = "float32", "bfloat16", "int32", "uint16"
 SCRATCH = {}
 for _n, _w, _d in (("IW", 160, f32), ("cA", 160, f32), ("c16", 128, f32), ("c32", 128, f32), ("cl", 64, f32), ("ri", 6, i32), ("cf", 16, f32),
                    ("Ib", 128, b16), ("nI", 128, f32), ("I2", 128, f32), ("nIb", 128, b16), ("B", 144, b16), ("Z0", 128, b16), ("Z1", 128, b16), ("zc", 64, b16), ("O32", 128, f32), ("A00", 128, f32), ("A01", 128, f32),
-                   ("A10", 128, f32), ("A11", 128, f32), ("H0", 128, f32), ("H1", 128, f32), ("m32", 32, f32), ("EM", 130, b16), ("DM", 8, b16),
-                   ("K4", 4, f32), ("TC", 14, f32), ("CV", 32, b16), ("CK", 32, b16), ("msk", 2048, b16), ("rv", 32, f32),
+                   ("A10", 128, f32), ("A11", 128, f32), ("H0", 128, f32), ("H1", 128, f32), ("m32", 32, f32), ("EM", 130, f32), ("DM", 8, b16),
+                   ("K8", 10, f32), ("O32e", 128, f32), ("kc", 2, b16), ("HH", 128, f32), ("TC", 14, f32), ("CV", 32, b16), ("CK", 32, b16), ("msk", 2048, b16), ("rv", 32, f32),
                    ("dl", 128, b16), ("ci", 132, i32), ("cfl", 132, f32), ("y1", 2048, f32), ("s", 8192, b16), ("finA", 132, f32), ("fin", 132, f32)):
     SCRATCH[_n] = ("sbuf", [128, _w], _d)
 SCRATCH["Pb"] = ("sbuf", [128, 8208], b16)
@@ -33,15 +38,15 @@ for _f in (0, 1):
                        ("Ou", 512, u16), ("U", 544, b16), ("unx", 512, b16), ("unb", 512, b16), ("pr", 512, b16), ("Lu", 4, u16),
                        ("g1", 64, b16), ("less", 32, b16), ("Lc", 32, u16), ("ev", 32, f32), ("en", 4, i32),
                        ("J", 2, u16), ("pro", 2, f32), ("sm", 2, f32), ("q", 32, f32), ("Cu", 32, u16), ("LT", 32, f32), ("L8", 32, f32), ("eq", 32, f32), ("mu", 32, f32),
-                       ("ex", 65, f32), ("d", 130, f32), ("T8", 8, u16), ("up", 128, b16), ("nw", 128, b16), ("X", 64, f32)):
+                       ("ex", 65, f32), ("d", 130, f32), ("em", 130, f32), ("x8", 16, f32), ("T8", 8, u16), ("up", 128, b16), ("nw", 128, b16), ("X", 64, f32)):
         SCRATCH[_n + str(_f)] = ("sbuf", [128, _w], _d)
     for _b in range(4):
         SCRATCH["ps%d%d" % (_f, _b)] = ("psum", [128, 512], f32)
-SEMAPHORES = ["eV", "eA", "eP", "eG", "sent", "ldc", "stv0", "stv1", "sto"] + ["ld%s%d" % (a, f) for a in "vg" for f in (0, 1)] \
+SEMAPHORES = ["eV", "eA", "eP", "eG", "sent", "ldc", "stv0", "stv1", "sto"] + ["ld%s%d" % (a, f) for a in "vgh" for f in (0, 1)] \
     + ["arr%s%d%d" % (a, t, f) for a in "ab" for t in range(1, RO) for f in (0, 1)]
 
-CY, GA, SCAT = 1.04, 1.56, 3.8
-LAT, NET = 160.0, 3000.0
+CY, GA, SCAT = 0.9, 1.56, 3.8
+LAT, OWN, NET, FIX = 130.0, 220.0, 2500.0, 2.0
 
 
 def build(T, dst_addr, emask, nen):
@@ -51,7 +56,7 @@ def build(T, dst_addr, emask, nen):
         ops.append({"e": eng, "fn": fn, "rd": rd, "wr": wr, "c": cost, "bk": bank, "sem": sem, "inc": inc})
 
     def V(fn, rd, wr, n=64, bank=None):
-        op("V", fn, rd, wr, max(n, 64) * CY + 15, bank)
+        op("V", fn, rd, wr, max(n, 64) * CY + FIX, bank)
 
     def ts(out, a, s1, s2, o0, o1, rd, wr, n=64, bank=None):
         if o1 is None:
@@ -78,7 +83,7 @@ def build(T, dst_addr, emask, nen):
         V(lambda e: e.transpose(out, a), rd, wr, n, bank)
 
     def mm(out, l, r, st, sp, rd, bank, n=64, wide=False):
-        op("P", lambda e: e.matmul(out, l, r, st, sp), rd, [], max(n, 64) * (4 if wide else 1) * CY * 0.7, bank)
+        op("P", lambda e: e.matmul(out, l, r, st, sp), rd, [], max(n, 64) * (4 if wide else 1) * CY * PEF, bank)
 
     def act(out, a, rd, wr, n, bias=0.0, scale=1.0, bank=None, func=F.Identity):
         op("A", lambda e: e.activation(out, a, func, bias=bias, scale=scale), rd, wr, n * CY + 65, bank)
@@ -104,12 +109,13 @@ def build(T, dst_addr, emask, nen):
     dma("S", T.ci[:, 64:128], T.cla[:], [], ["ci1"], "ldc", 2200)
     dma("S", T.ci[:, 128:132], T.lit[:], [], ["ci2"], "ldc", 2200)
     for f in (0, 1):
-        for nm, src, buf, c0 in (("g", T.gen, T["gi%d" % f], 0), ("v", T.val, T["V%d" % f], PAD)):
+        for nm, src, buf, c0, a, b, at in (("g", T.gen, T["gi%d" % f], 0, 0, 1024, 2200), ("h", T.gen, T["gi%d" % f], 0, 1024, 2048, 3000),
+                                           ("v", T.val, T["V%d" % f], PAD, 0, 4096, 4200)):
             for j in range(8):
                 gr = 2 * (j // 2) + f
-                dma("A" if f == 0 and j % 2 else "S", buf[16 * j:16 * j + 16, c0:], src[16 * gr:16 * gr + 16, :],
+                dma("A" if f == 0 and j % 2 else "S", buf[16 * j:16 * j + 16, c0 + a:c0 + b], src[16 * gr:16 * gr + 16, a:b],
                     ["ldv0%d" % z for z in range(8)] if f else [], ["ld%s%d%d" % (nm, f, j)],
-                    "ld%s%d" % (nm, f), 2500 + 2500 * (nm == "v") + 300 * j)
+                    "ld%s%d" % (nm, f), at + (300 if nm == "v" else 150) * j)
     io(T.ri[:, 0:1], [[0, 1]], 0, 1, ["ri"], 1, False)
     io(T.cA[:], [[1, 160]], -16, 0, ["cA"], 160)
     io(T.c16[:], [[16, 8], [0, 16]], 0, 0, ["c16"], 128)
@@ -134,6 +140,7 @@ def build(T, dst_addr, emask, nen):
             o = 16 - 16 * (y - x)
             ts(T["A%d%d" % (x, y)][:], T.IW[:, o:o + 128], half[x], None, A.mult, None, ["IW", "h0", "h1"], ["A%d%d" % (x, y)], 128)
         tt(T["H%d" % x][:], T["A%d0" % x][:], T["A%d1" % x][:], A.add, ["A%d0" % x, "A%d1" % x], ["H%d" % x], 256)
+    tt(T.HH[:], T.H0[:], T.H1[:], A.add, ["H0", "H1"], ["HH"], 256)
     cp(T.Ib[:], T.IW[:, 16:144], ["IW"], ["Ib"], 128)
     ts(T.nIb[:], T.IW[:, 16:144], -1.0, None, A.mult, None, ["IW"], ["nIb"], 128)
     ts(T.nI[:], T.IW[:, 16:144], -1.0, None, A.mult, None, ["IW"], ["nI"], 128)
@@ -147,14 +154,18 @@ def build(T, dst_addr, emask, nen):
     ts(T.m32[:], T.cA[:, 16:48], c31, None, A.is_equal, None, ["cA", "cf"], ["m32"])
     ms(T.EM[:], 0.0, ["EM"])
     for q in (0, 1):
-        ts(T.EM[:, 65 * q:65 * q + 64], T.cl[:], cf[:, 8 + q:9 + q], 2.0 ** 28, A.is_ge, A.mult, ["cl", "own0", "own1", "EM"], ["EM%d" % q])
+        ts(T.EM[:, 65 * q:65 * q + 64], T.cl[:], cf[:, 8 + q:9 + q], 2.0 ** 15, A.is_ge, A.mult, ["cl", "own0", "own1", "EM"], ["EM%d" % q])
     ts(T.DM[:], T.c16[:, 0:128:16], cp_, None, A.add, None, ["c16", "cf"], ["DM"])
     ts(cf[:, 12:16], T.c16[:, 0:64:16], cf[:, 10:11], -1.0, A.add, A.mult, ["c16", "dm0"], ["k40"])
-    ts(T.K4[:], cf[:, 12:16], 4096.5, None, A.add, None, ["k40"], ["K4"])
+    for x in (0, 1):
+        ts(T.K8[:, 8 + x:9 + x], half[1 - x], -16384.0, 4096.5, A.mult, A.add, ["h0", "h1"], ["kh%d" % x])
+        ts(T.K8[:, 4 * x:4 * x + 4], cf[:, 12:16], T.K8[:, 8 + x:9 + x], None, A.add, None, ["k40", "kh%d" % x], ["K8%d" % x])
     ts(T.CV[:], T.c16[:, 0:32], -1.0, cf[:, 11:12], A.mult, A.add, ["c16", "cv0"], ["CV"])
-    ts(T.TC[:, 12:14], T.c16[:, 0:32:16], cp_, -8.0, A.add, A.mult, ["c16", "cf"], ["TCb"])
+    ts(T.TC[:, 12:14], T.c16[:, 0:32:16], cp_, -1.0, A.add, A.mult, ["c16", "cf"], ["TCb"])
+    ts(T.O32e[:], T.c32[:], c32r, 0.125, A.is_equal, A.mult, ["c32", "cf"], ["O32e"], 128)
+    ms(T.kc[:], -512.0, ["kc"])
     for t in range(RO):
-        ts(T.TC[:, 2 * t:2 * t + 2], T.TC[:, 12:14], 8.0 * (1024 * AT[t] + 511), None, A.add, None, ["TCb"], ["TC%d" % t])
+        ts(T.TC[:, 2 * t:2 * t + 2], T.TC[:, 12:14], 1024.0 * AT[t] + 1023, None, A.add, None, ["TCb"], ["TC%d" % t])
     ms(T.rv[:], 1.0, ["rv"]); ms(T.rv[:, 0:32:16], -BIG, ["rv"])
     nm_ = max(512, PIECE * 256)
     ms(T.msk[:, 0:nm_], 1.0, ["msk"], nm_ // 2); ms(T.msk[:, 0:nm_:16], 0.0, ["msk"])
@@ -186,15 +197,14 @@ def build(T, dst_addr, emask, nen):
         ts(q_[:, 8:10], W[:, 576:578], M2, -M2, A.add, A.add, [k("in0a")], [k("r")])
         tt(q_[:, 10:12], q_[:, 8:10], W[:, 576:578], A.subtract, [k("r"), k("in0a")], [k("r1")])
         tt(W[:, 578:580], q_[:, 10:12], q_[:, 8:10], A.add, [k("r"), k("r1")], [k("in0b")])
-        ts(q_[:, 0:2], T.TC[:, 0:2], 0.125, None, A.mult, None, ["TC0"], [k("T")])
-        gl = ["ldg%d%d" % (f, j) for j in range(8)]
+        ts(q_[:, 0:2], T.TC[:, 0:2], -512.0, None, A.add, None, ["TC0"], [k("T")])
         P = B("P")
         first = len(ops)
         for i in range(4):
             ev, od = P[:, 1024 * i:1024 * i + 1024:2], P[:, 1024 * i + 1:1024 * i + 1024:2]
             y = T.y1[:, 512 * i:512 * i + 512]
             b = 3 * (i % 2)
-            ts(ev, B("gi")[:, 512 * i:512 * i + 512], OFF, None, A.add, None, gl, [k("Pe%d" % i)], 512)
+            ts(ev, B("gi")[:, 512 * i:512 * i + 512], OFF, None, A.add, None, ["ld%s%d%d" % ("gh"[i // 2], f, j) for j in range(8)], [k("Pe%d" % i)], 512)
             how = PB[4 * f + i]
             if how == "a":
                 act(y, ev, [k("Pe%d" % i)], ["y%d" % i], 512, M4, 2.0)
@@ -255,7 +265,7 @@ def build(T, dst_addr, emask, nen):
             gat(B("I")[:, 16 * a:16 * b], B("P")[:, 0:4096].indirect(B("Lc")[:, a:b]), PK + [k("Lc")], [k("I%d" % u)], 16 * (b - a))
             tr(Wc(16 * a, 16 * b), B("I")[:, 16 * a:16 * b], [k("I%d" % u)], [sb("O%d" % u)], 16 * (b - a))
             ts(B("Ou")[:, 16 * a:16 * b], Wc(16 * a, 16 * b), 0.5, None, A.add, None, [sb("O%d" % u)], [k("Ou_%d_" % z) for z in range(a, b)], 16 * (b - a))
-        a0 = 0
+        a0 = held = 0
         UK = []
         for ci, n in enumerate(CHUNKS):
             nv = VSHARE.get((t, f, ci), 0)
@@ -296,7 +306,11 @@ def build(T, dst_addr, emask, nen):
                     scan(T.s[:, 256 * a:256 * b], B("w")[:, 256 * a:256 * b], T.Pb[:, 256 * a:256 * b], A.max, A.min,
                          lk("w", a, b) + ["Pb_%d" % z for z in range(max(a - 1, 0), b)] + ["Pb0"], ["s_%d" % z for z in range(a, b)], 128 * (b - a))
                     ops[-1]["bulk"] = 1
-            db = 3 * ((len(CHUNKS) - 1 - ci) % 2)
+            if ci in JOIN:
+                held, a0 = held + n, a0 + n
+                continue
+            a0, n, held = a0 - held, n + held, 0
+            db = 3 * (len([z for z in range(ci + 1, len(CHUNKS)) if z not in JOIN]) % 2)
             dps = ps[db][:, 16 * a0:16 * (a0 + n)]
             mm(dps, T.Ib[:], T.Mx[:, 16 * a0:16 * (a0 + n)], True, False, ["Mx_%d" % z for z in range(a0, a0 + n)] + ["Ib"], bk[db], 16 * n)
             mm(dps, T.nIb[:], T.s[:, 256 * a0 + 15:256 * (a0 + n):16], False, True, ["s_%d" % z for z in range(a0, a0 + n)] + ["nIb"], bk[db], 16 * n)
@@ -330,51 +344,50 @@ def build(T, dst_addr, emask, nen):
         tr(B("LT")[:], ps[2][:, 64:96], [], [k("LT")], 64, bk[2])
         for q in (0, 1):
             ts(B("L8")[:, 16 * q:16 * q + 16], B("LT")[:, 16 * q:16 * q + 16], Wc(576 + q, 577 + q), pro[:, q:q + 1], A.subtract, A.mult, [k("LT"), k("pro")] + IN, [k("L8%d" % q)])
-        for q in (0, 1):
-            tt(B("pr")[:, q:512:2], Vw.indirect(B("Cu")[:, 16 * q:16 * q + 16]), B("unb")[:, 256 * q:256 * q + 256], A.mult,
-               VK + [k("Cu"), k("unb")], [k("pr%d" % q)], 50 + 256 * GA)
+            ts(B("L8")[:, 16 * q:16 * q + 16], B("L8")[:, 16 * q:16 * q + 16], 1.0 / 8192, Wc(576 + q, 577 + q), A.mult, A.add, [k("L8%d" % q)] + IN, [k("L8%d" % q)])
         mm(ps[1][:, 32:64], T.Ib[:], T.CK[:], True, False, ["Ib", "CK"], bk[1])
-        for p in range(16):
-            mm(ps[1][:, 32:64], T.B[:, 16 - p:144 - p], B("pr")[:, 32 * p:32 * p + 32], False, p == 15, ["B", k("pr0"), k("pr1")], bk[1])
+        for a, b in zip([0] + SUMS, SUMS + [16]):
+            for q in (0, 1):
+                tt(B("pr")[:, 32 * a + q:32 * b:2], Vw.indirect(B("Cu")[:, 16 * q + a:16 * q + b]), B("unb")[:, 256 * q + 16 * a:256 * q + 16 * b], A.mult,
+                   VK + [k("Cu"), k("unb")], [k("pr%d_%d_" % (q, p)) for p in range(a, b)], 50 + 16 * (b - a) * GA)
+            for p in range(a, b):
+                mm(ps[1][:, 32:64], T.B[:, 16 - p:144 - p], B("pr")[:, 32 * p:32 * p + 32], False, p == 15, ["B", k("pr0_%d_" % p), k("pr1_%d_" % p)], bk[1])
         for q in (0, 1):
             V(lambda e, q=q: e.tensor_reduce(B("sm")[:, q:q + 1], ps[1][:, 32 + q:64:2], AxisListType.X, A.max), [], [k("sm%d" % q)], 64, bk[1])
         for q in (0, 1):
-            ts(B("eq")[:, 16 * q:16 * q + 16], ps[1][:, 32 + q:64:2], B("sm")[:, q:q + 1], 1.0 / 8192, A.is_equal, A.mult, [k("sm%d" % q)], [k("eq%d" % q)], 64, bk[1])
+            ts(B("eq")[:, 16 * q:16 * q + 16], ps[1][:, 32 + q:64:2], B("sm")[:, q:q + 1], None, A.is_equal, None, [k("sm%d" % q)], [k("eq%d" % q)], 64, bk[1])
         tt(B("mu")[:], B("eq")[:], B("L8")[:], A.mult, [k("eq0"), k("eq1"), k("L80"), k("L81")], [k("mu")])
-        scan(B("eq")[:], T.msk[:, 0:32], B("mu")[:], A.mult, A.add, ["msk", k("mu")], [k("eq0"), k("eq1")])
-        tt(Sc(64, 66), B("eq")[:, 15:32:16], Wc(576, 578), A.add, [k("eq0"), k("eq1")] + IN, [sb("l")])
-        LK = [sb("l")]
+        for q in (0, 1):
+            red(Sc(64 + q, 65 + q), B("mu")[:, 16 * q:16 * q + 16], A.add, [k("mu")], [sb("l%d" % q)])
+        LK = [sb("l0"), sb("l1")]
         ts(q_[:, 8:10], Sc(64, 66), M2, -M2, A.add, A.add, LK, [k("r")])
         for q in (0, 1):
-            ts(B("ex")[:, 32 * q:32 * q + 32], T.m32[:], Sc(64 + q, 65 + q), pro[:, q:q + 1], A.mult, A.mult, ["m32", sb("l"), k("pro")], [k("ex%d" % q)])
+            ts(B("ex")[:, 32 * q:32 * q + 32], T.m32[:], Sc(64 + q, 65 + q), pro[:, q:q + 1], A.mult, A.mult, ["m32", sb("l%d" % q), k("pro")], [k("ex%d" % q)])
         tt(q_[:, 10:12], q_[:, 8:10], Sc(64, 66), A.subtract, [k("r")] + LK, [k("r1")])
         tt(Sc(66, 68), q_[:, 10:12], q_[:, 8:10], A.add, [k("r"), k("r1")], [sb("lp")])
         send("b", 64, 68, [sb("lp")] + LK)
-        tt(q_[:, 12:14], q_[:, 8:10], pro[:], A.mult, [k("r"), k("pro")], [k("ep")])
-        tt(q_[:, 16:20], Sc(64, 68), T.K4[:], A.add, LK + [sb("lp"), "K4"], [k("A2")])
+        mm(ps[3][:, 0:65], T.O32[:], B("ex")[:], True, True, ["O32", k("ex0"), k("ex1"), k("exp")], bk[3], 65, True)
+        mm(ps[0][:, 0:8], T.Ib[:], T.DM[:], True, False, ["Ib", "DM"], bk[0])
+        x8 = B("x8")
         for q in (0, 1):
-            o = ps[3][:, 65 * q:65 * q + 65]
-            mm(o, T.Ib[:], T.EM[:, 65 * q:65 * q + 65], True, False, ["Ib", "EM", "EM0", "EM1"], bk[3])
-            mm(o, T.O32[:], B("ex")[:], False, True, ["O32", k("ex0"), k("ex1"), k("exp")], bk[3], 65, True)
+            ts(B("em")[:, 65 * q:65 * q + 65], T.EM[:, 65 * q:65 * q + 65], q_[:, 8 + q:9 + q], pro[:, q:q + 1], A.subtract, A.mult, ["EM", "EM0", "EM1", k("r"), k("pro")], [k("em%d" % q)], 65)
+            tt(x8[:, 4 * q:4 * q + 4], Sc(64, 68), T.K8[:, 4 * q:4 * q + 4], A.add, LK + [sb("lp"), "K80", "K81"], [k("A2%d" % q)])
         for q in (0, 1):
-            ts(B("d")[:, 65 * q:65 * q + 65], ps[3][:, 65 * q:65 * q + 65], q_[:, 12 + q:13 + q], None, A.subtract, None, [k("ep")], [k("d%d" % q)], 65, bk[3])
+            tt(B("d")[:, 65 * q:65 * q + 65], ps[3][:, 0:65], B("em")[:, 65 * q:65 * q + 65], A.add, [k("em%d" % q)], [k("d%d" % q)], 65, bk[3])
         for q in (0, 1):
             red(q_[:, 14 + q:15 + q], B("d")[:, 65 * q:65 * q + 65], A.min, [k("d%d" % q)], [k("mn%d" % q)], True)
-            ts(q_[:, 20 + q:24:2], q_[:, 16 + q:20:2], q_[:, 14 + q:15 + q], 4096.0, A.min, A.max, [k("mn%d" % q), k("A2")], [k("X%d" % q)])
-        for x in (0, 1):
-            o = ps[3][:, 136 + 4 * x:140 + 4 * x]
-            mm(o, T.Ib[:], T.DM[:, 4 * x:4 * x + 4], True, False, ["Ib", "DM"], bk[3])
-            mm(o, T["H%d" % x][:], q_[:, 20:24], False, True, ["H0", "H1", k("X0"), k("X1")], bk[3], 4, True)
-        ts(B("T8")[:], ps[3][:, 136:144], -4096.0, None, A.add, None, [], [k("T8")], 64, bk[3])
+            ts(x8[:, 8 + q:16:2], x8[:, q:8:2], q_[:, 14 + q:15 + q], 4096.0, A.min, A.max, [k("mn%d" % q), k("A20"), k("A21")], [k("X%d" % q)])
+        mm(ps[0][:, 0:8], T.HH[:], x8[:, 8:16], False, True, ["HH", k("X0"), k("X1")], bk[0], 8, True)
+        ts(B("T8")[:], ps[0][:, 0:8], -8192.0, None, A.add, None, [], [k("T8")], 64, bk[0])
         tt(B("up")[:], Vw.indirect(B("T8")[:, 0:8]), T.dl[:], A.add, VK + [k("T8"), "dl"], [k("up")], 50 + 128 * GA)
         ts(B("nw")[:], B("up")[:], 0.0, 255.0, A.max, A.min, [k("up")], [k("nw")])
         cp(Vw.indirect(B("T8")[:, 0:8]), B("nw")[:], VK[1:] + [k("nw"), k("T8")], [k("V")], 50 + 128 * SCAT)
         if t + 1 < RO:
+            mm(ps[2][:, 96:97], T.Ib[:], T.kc[:, 0:1], True, False, ["Ib", "kc"], bk[2])
             for q in (0, 1):
-                mm(ps[2][:, 96:97], T.O32[:], pro[:, q:q + 1], q == 0, q == 1, ["O32", k("pro")], bk[2], 1, True)
-            ts(q_[:, 24:25], ps[2][:, 96:97], -4096.0, M16K, A.add, A.add, [], [k("a1")], 64, bk[2])
-            ts(q_[:, 25:26], q_[:, 24:25], -M16K, ps[2][:, 96:97], A.add, A.subtract, [k("a1")], [k("a2")], 64, bk[2])
-            ts(q_[:, 0:2], T.TC[:, 2 * t + 2:2 * t + 4], q_[:, 25:26], 0.125, A.subtract, A.mult, ["TC%d" % (t + 1), k("a2")], [k("T")])
+                mm(ps[2][:, 96:97], T.O32e[:], pro[:, q:q + 1], False, q == 1, ["O32e", k("pro")], bk[2], 1, True)
+            ts(q_[:, 24:25], ps[2][:, 96:97], M2K, -M2K, A.add, A.add, [], [k("a1")], 64, bk[2])
+            ts(q_[:, 0:2], T.TC[:, 2 * t + 2:2 * t + 4], ps[2][:, 96:97], q_[:, 24:25], A.add, A.subtract, ["TC%d" % (t + 1), k("a1")], [k("T")], 64, bk[2])
         else:
             tr(B("X")[:], Sc(0, 64), [sb("c"), sb("C")], [k("XX")])
             for j in (0, 1):
@@ -398,8 +411,16 @@ def build(T, dst_addr, emask, nen):
     phase_setup(0)
     phase_setup(1)
     for t in range(RO):
+        first = len(ops)
         phase(t, 0)
+        if t + 1 == RO:
+            late = [o for o in ops[first:] if o["e"] == "V" and not o.get("bulk")]
+            for o in late[DEFER:]:
+                o["bulk"] = 1.5
+        second = len(ops)
         phase(t, 1)
+        for i in range(first, len(ops)):
+            ops[i]["k"] = i - (first if i < second else second)
     return ops
 
 
@@ -436,7 +457,9 @@ def schedule(ops):
     pri = [0.0] * n
     for i in range(n - 1, -1, -1):
         o = ops[i]
-        pri[i] = o["c"] + o.get("lat", 0) + max([pri[j] + (LAT if i in ops[j]["hard"] else 0) for j in succ[i]] + [0])
+        pri[i] = o["c"] + o.get("lat", 0) + max([pri[j] + ((OWN if ops[j]["e"] == o["e"] else LAT) if i in ops[j]["hard"] else 0) for j in succ[i]] + [0])
+    for i, o in enumerate(ops):
+        pri[i] += NUDGE * (((o.get("k", 0) + 1) * (2 * SEED + 1) * 2654435761 >> 8) % 1000 / 1000.0)
     left = [len(o["hard"] | o["soft"]) for o in ops]
     rdy = [0.0] * n
     free = {e: 0.0 for e in "VAPGSN"}
@@ -472,7 +495,7 @@ def schedule(ops):
         fin = done + o.get("lat", 0)
         end = max(end, fin)
         for j in succ[i]:
-            rdy[j] = max(rdy[j], fin + LAT if i in ops[j]["hard"] else done)
+            rdy[j] = max(rdy[j], fin + (OWN if ops[j]["e"] == e else LAT) if i in ops[j]["hard"] else done)
             left[j] -= 1
             if left[j] == 0:
                 cand[ops[j]["e"]].append(j)

@@ -3,107 +3,120 @@ from concourse.mybir import AluOpType as A, AxisListType, ActivationFunctionType
 RO = 6
 MT = [16, 12, 20, 14, 24, 10]
 AT = [8, 10, 7, 9, 6, 11]
-PAD = 128
+PAD = 144
 NV = PAD + 4096
 OFF = PAD - 0.5
-M2, M4, M2K = 1.5 * 2 ** 24, 1.5 * 2 ** 25, 1.5 * 2 ** 34
-BIG = 1.0e9
+CB = 2048.0
+M2, M4, M2K, M4K = 1.5 * 2 ** 24, 1.5 * 2 ** 25, 1.5 * 2 ** 34, 1.5 * 2 ** 35
+BIG = 8192.0
 CHUNKS = [4, 4, 4, 4, 4, 4, 4, 2, 2]
 PIECE = 2
 SHORT = 1
 IMG = [8]
-SUMS = []
-PEF = 0.5
-DEFER = 14
-NUDGE, SEED = 0.0, 0
+IMGB = [0, 0, 0]
 JOIN = (0, 1, 3, 4)
-VSHARE = {(RO - 1, 1, 4): 1, (RO - 1, 1, 5): 1, (RO - 1, 1, 6): 1}
-UNIT_ACT = 6
+VSHARE = {}
+UNIT_ACT = {}
+UNIT_DEF = 6
+IMG_ACT = set()
 PB = "aaaaqqqq"
+CONB = 0.5
+P1B = 1
+DEFER = 14
+WAIT = {}
 LOOK, BULK = 40.0, 20000.0
 
-f32, b16, i32, u16 = "float32", "bfloat16", "int32", "uint16"
+IMG_ACT, WAIT, SHORT, JOIN, IMGB, DEFER, P1B, CONB, PB = {(0, 0)}, {"nr": 320}, 2, (0, 1, 3, 4, 7), [1.2], 22, 0, 1, "aaaaqqpp"
+VSHARE = {(RO - 1, 1, 2): 1, (RO - 1, 1, 4): 1}
+f32, b16, f16, i32, u16 = "float32", "bfloat16", "float16", "int32", "uint16"
 SCRATCH = {}
-for _n, _w, _d in (("IW", 160, f32), ("cA", 160, f32), ("c16", 128, f32), ("c32", 128, f32), ("cl", 64, f32), ("ri", 6, i32), ("cf", 16, f32),
-                   ("Ib", 128, b16), ("nI", 128, f32), ("I2", 128, f32), ("nIb", 128, b16), ("B", 144, b16), ("Z0", 128, b16), ("Z1", 128, b16), ("zc", 64, b16), ("O32", 128, f32), ("A00", 128, f32), ("A01", 128, f32),
-                   ("A10", 128, f32), ("A11", 128, f32), ("H0", 128, f32), ("H1", 128, f32), ("m32", 32, f32), ("EM", 130, f32), ("DM", 8, b16),
-                   ("K8", 10, f32), ("O32e", 128, f32), ("kc", 2, b16), ("HH", 128, f32), ("TC", 14, f32), ("CV", 32, b16), ("CK", 32, b16), ("msk", 2048, b16), ("rv", 32, f32),
-                   ("dl", 128, b16), ("ci", 132, i32), ("cfl", 132, f32), ("y1", 2048, f32), ("s", 8192, b16), ("finA", 132, f32), ("fin", 132, f32)):
+for _n, _w, _d in (("IW", 164, f32), ("Zr", 128, f32), ("km", 512, b16), ("k1", 512, b16), ("c16", 128, f32), ("c32", 128, f32), ("cl", 64, f32), ("ri", 6, i32), ("cf", 32, f32),
+                   ("Ib", 128, b16), ("nI", 128, f32), ("I2", 128, f32), ("nIb", 128, b16), ("B", 144, b16), ("Z0", 128, b16), ("Z1", 128, b16), ("zc", 64, b16),
+                   ("AM", 512, f32), ("AH", 512, f16), ("GM", 512, f16), ("HM", 256, f32), ("SM", 256, f32), ("EMf", 128, f32), ("EM", 128, b16), ("DM", 8, b16),
+                   ("O32e", 128, f32), ("kc", 2, b16), ("TC", 14, f32), ("CV", 38, b16), ("CK", 38, b16), ("msk", 512, b16), ("rv", 38, f32), ("rE", 38, f32),
+                   ("KR", 64, f32), ("KH", 64, f32), ("SP", 132, f32), ("dl", 128, b16), ("ci", 132, i32), ("cfl", 132, f32), ("y1", 2048, f32), ("s", 8192, b16),
+                   ("finA", 132, f32), ("fin", 132, f32), ("Pb", 8208, b16), ("E", 1024, b16), ("Mx", 512, b16), ("I", 512, f32), ("Ih", 512, f16), ("Wh", 512, f16)):
     SCRATCH[_n] = ("sbuf", [128, _w], _d)
-SCRATCH["Pb"] = ("sbuf", [128, 8208], b16)
-SCRATCH["E"] = ("sbuf", [128, 2048], b16)
-SCRATCH["Mx"] = ("sbuf", [128, 512], b16)
 for _f in (0, 1):
-    for _n, _w, _d in (("P", 4096, f32), ("V", NV, b16), ("gi", 2048, i32), ("w", 8192, b16), ("W", 584 * RO, f32), ("SB", 72 * RO, f32), ("I", 512, f32),
+    for _n, _w, _d in (("P", 4096, f32), ("V", NV, b16), ("gi", 2048, i32), ("w", 8192, b16), ("W", 584 * RO + 584, f32), ("SB", 64 * RO, f16), ("Wa", 64 * RO + 64, f16), ("Xh", 64, f16), ("D", 164 * RO, f32),
                        ("Ou", 512, u16), ("U", 544, b16), ("unx", 512, b16), ("unb", 512, b16), ("pr", 512, b16), ("Lu", 4, u16),
-                       ("g1", 64, b16), ("less", 32, b16), ("Lc", 32, u16), ("ev", 32, f32), ("en", 4, i32),
-                       ("J", 2, u16), ("pro", 2, f32), ("sm", 2, f32), ("q", 32, f32), ("Cu", 32, u16), ("LT", 32, f32), ("L8", 32, f32), ("eq", 32, f32), ("mu", 32, f32),
-                       ("ex", 65, f32), ("d", 130, f32), ("em", 130, f32), ("x8", 16, f32), ("T8", 8, u16), ("up", 128, b16), ("nw", 128, b16), ("X", 64, f32)):
+                       ("g1", 32, b16), ("less", 32, b16), ("Lc", 32, u16), ("ev", 38, f32), ("J", 2, u16), ("q", 8, f32), ("Cu", 32, u16), ("LT", 64, f32),
+                       ("Eb", 38, f32), ("nr", 38, f32), ("TT", 32, f32), ("Y", 132, f32), ("T8", 8, u16), ("up", 128, b16), ("X", 64, f32)):
         SCRATCH[_n + str(_f)] = ("sbuf", [128, _w], _d)
     for _b in range(4):
         SCRATCH["ps%d%d" % (_f, _b)] = ("psum", [128, 512], f32)
 SEMAPHORES = ["eV", "eA", "eP", "eG", "sent", "ldc", "stv0", "stv1", "sto"] + ["ld%s%d" % (a, f) for a in "vgh" for f in (0, 1)] \
     + ["arr%s%d%d" % (a, t, f) for a in "ab" for t in range(1, RO) for f in (0, 1)]
 
-CY, GA, SCAT = 0.9, 1.56, 3.8
-LAT, OWN, NET, FIX = 130.0, 220.0, 2500.0, 2.0
+CY, GA, SCAT, PEF = 0.9, 1.56, 3.8, 0.5
+LAT, OWN, NET = 130.0, 220.0, 2300.0
 
 
 def build(T, dst_addr, emask, nen):
     ops = []
 
-    def op(eng, fn, rd, wr, cost, bank=None, sem=None, inc=1):
-        ops.append({"e": eng, "fn": fn, "rd": rd, "wr": wr, "c": cost, "bk": bank, "sem": sem, "inc": inc})
+    def op(eng, fn, rd, wr, cyc, bank=None, sem=None, inc=1, gn=0, sn=0, fx=0.0):
+        c = NET if eng == "N" else (cyc * (PEF if eng == "P" else 1) + gn * GA + sn * SCAT) * CY + fx
+        ops.append({"e": eng, "fn": fn, "rd": rd, "wr": wr, "c": c, "bk": bank, "sem": sem, "inc": inc, "cyc": cyc, "gn": gn, "sn": sn, "fx": fx})
 
-    def V(fn, rd, wr, n=64, bank=None):
-        op("V", fn, rd, wr, max(n, 64) * CY + FIX, bank)
-
-    def ts(out, a, s1, s2, o0, o1, rd, wr, n=64, bank=None):
-        if o1 is None:
-            V(lambda e: e.tensor_scalar(out, a, s1, None, o0), rd, wr, n, bank)
+    def V(fn, rd, wr, n=64, bank=None, gn=0, sn=0):
+        if gn or sn:
+            op("V", fn, rd, wr, 0, bank, gn=gn, sn=sn, fx=50.0)
         else:
-            V(lambda e: e.tensor_scalar(out, a, s1, s2, o0, o1), rd, wr, n, bank)
+            op("V", fn, rd, wr, max(n, 64), bank, fx=2.0)
 
-    def tt(out, a, b, o, rd, wr, n=64, bank=None):
-        V(lambda e: e.tensor_tensor(out, a, b, o), rd, wr, n, bank)
+    def ts(out, a, s1, s2, o0, o1, rd, wr, n=64, bank=None, gn=0):
+        if o1 is None:
+            V(lambda e: e.tensor_scalar(out, a, s1, None, o0), rd, wr, n, bank, gn)
+        else:
+            V(lambda e: e.tensor_scalar(out, a, s1, s2, o0, o1), rd, wr, n, bank, gn)
 
-    def cp(out, a, rd, wr, n=64, bank=None):
-        V(lambda e: e.tensor_copy(out, a), rd, wr, n, bank)
+    def tt(out, a, b, o, rd, wr, n=64, bank=None, gn=0):
+        V(lambda e: e.tensor_tensor(out, a, b, o), rd, wr, n, bank, gn)
+
+    def cp(out, a, rd, wr, n=64, bank=None, gn=0, sn=0):
+        V(lambda e: e.tensor_copy(out, a), rd, wr, n, bank, gn, sn)
 
     def ms(out, c, wr, n=64):
         V(lambda e: e.memset(out, c), [], wr, n)
 
-    def scan(out, d0, d1, o0, o1, rd, wr, n=64, bank=None):
-        V(lambda e: e.tensor_tensor_scan(out, d0, d1, 0.0, o0, o1), rd, wr, n, bank)
-
-    def red(out, a, o, rd, wr, ab=False):
-        V(lambda e: e.tensor_reduce(out, a, AxisListType.X, o, apply_absolute_value=ab), rd, wr)
+    def scan(out, d0, d1, o0, o1, rd, wr, n=64, bank=None, init=0.0):
+        V(lambda e: e.tensor_tensor_scan(out, d0, d1, init, o0, o1), rd, wr, n, bank)
 
     def tr(out, a, rd, wr, n=64, bank=None):
         V(lambda e: e.transpose(out, a), rd, wr, n, bank)
 
     def mm(out, l, r, st, sp, rd, bank, n=64, wide=False):
-        op("P", lambda e: e.matmul(out, l, r, st, sp), rd, [], max(n, 64) * (4 if wide else 1) * CY * PEF, bank)
+        op("P", lambda e: e.matmul(out, l, r, st, sp), rd, [], max(n, 64) * (4 if wide else 1), bank)
 
     def act(out, a, rd, wr, n, bias=0.0, scale=1.0, bank=None, func=F.Identity):
-        op("A", lambda e: e.activation(out, a, func, bias=bias, scale=scale), rd, wr, n * CY + 65, bank)
+        op("A", lambda e: e.activation(out, a, func, bias=bias, scale=scale), rd, wr, n, bank, fx=65.0)
 
-    def gat(out, a, rd, wr, n):
-        op("A", lambda e: e.activation(out, a, F.Copy), rd, wr, n * GA * CY + 65)
-        ops[-1]["g"] = 1
+    def gat(out, a, rd, wr, n, bias=None):
+        if bias is None:
+            op("A", lambda e: e.activation(out, a, F.Copy), rd, wr, 0, gn=n, fx=65.0)
+        else:
+            op("A", lambda e: e.activation(out, a, F.Identity, bias=bias), rd, wr, 0, gn=n, fx=65.0)
 
     def io(out, pat, base, cm, wr, n, flag=True):
         if flag:
-            op("G", lambda e: e.iota(out, pat, base, cm, allow_small_or_imprecise_dtypes=True), [], wr, 130 + 2 * n * CY)
+            op("G", lambda e: e.iota(out, pat, base, cm, allow_small_or_imprecise_dtypes=True), [], wr, 2 * n, fx=130.0)
         else:
-            op("G", lambda e: e.iota(out, pat, base, cm), [], wr, 130 + 2 * n * CY)
+            op("G", lambda e: e.iota(out, pat, base, cm), [], wr, 2 * n, fx=130.0)
 
     def move(out, a, n, rd, wr):
-        op("G", lambda e: e.affine_select(out, a, [[0, n]], A.is_ge, 0.0, 0, 0), rd, wr, 170 + 2 * n * CY)
+        op("G", lambda e: e.affine_select(out, a, [[0, n]], A.is_ge, 0.0, 0, 0), rd, wr, 2 * n, fx=170.0)
+
+    def put(out, a, pat, base, val, rd, wr, n=128):
+        op("G", lambda e: e.affine_select(out, a, pat, A.not_equal, val, base, 1), rd, wr, 2 * n, fx=170.0)
 
     def dma(q, out, a, rd, wr, sem, lat):
-        op(q, lambda e: e.dma_start(out, a), rd, wr, 100, "dma" + q, sem, 16)
+        op(q, lambda e: e.dma_start(out, a), rd, wr, 0, "dma" + q, sem, 16, fx=100.0)
         ops[-1]["lat"] = lat
+
+    def later(first, how=1):
+        for o in ops[first:]:
+            o["bulk"] = how
 
     dma("S", T.ci[:, 0:64], T.par[:], [], ["ci0"], "ldc", 2200)
     dma("S", T.ci[:, 64:128], T.cla[:], [], ["ci1"], "ldc", 2200)
@@ -117,61 +130,81 @@ def build(T, dst_addr, emask, nen):
                     ["ldv0%d" % z for z in range(8)] if f else [], ["ld%s%d%d" % (nm, f, j)],
                     "ld%s%d" % (nm, f), at + (300 if nm == "v" else 150) * j)
     io(T.ri[:, 0:1], [[0, 1]], 0, 1, ["ri"], 1, False)
-    io(T.cA[:], [[1, 160]], -16, 0, ["cA"], 160)
     io(T.c16[:], [[16, 8], [0, 16]], 0, 0, ["c16"], 128)
-    io(T.c32[:], [[32, 4], [0, 32]], 0, 0, ["c32"], 128)
-    io(T.cl[:], [[16, 2], [32, 2], [1, 16]], 0, 0, ["cl"], 64)
-    io(T.CK[:], [[-1, 16], [0, 2]], 15, 0, ["CK"], 32)
-    for j, m in enumerate((15, 16, 112, 96, 31)):
-        ts(T.ri[:, j + 1:j + 2], T.ri[:, 0:1], m, None, A.bitwise_and, None, ["ri"], ["ri%d" % j])
-    cf = T.cf
-    cp(cf[:, 0:6], T.ri[:], ["ri"] + ["ri%d" % j for j in range(5)], ["cf"])
-    cr, cp_, ch, c16r, c32r, c31 = [cf[:, j:j + 1] for j in range(6)]
-    ts(cf[:, 6:7], ch, 1.0 / 16, None, A.mult, None, ["cf"], ["h1"])
-    ts(cf[:, 7:8], ch, -1.0 / 16, 1.0, A.mult, A.add, ["cf"], ["h0"])
-    ts(cf[:, 8:9], ch, 2.0, cp_, A.mult, A.add, ["cf"], ["own0"])
-    ts(cf[:, 9:10], cf[:, 8:9], 16.0, None, A.add, None, ["own0"], ["own1"])
-    ts(cf[:, 10:11], ch, 4.0, cp_, A.mult, A.add, ["cf"], ["dm0"])
-    ts(cf[:, 11:12], cp_, -32.0, 1008.0, A.mult, A.add, ["cf"], ["cv0"])
-    ts(T.IW[:], T.cA[:], cr, None, A.is_equal, None, ["cA", "cf"], ["IW"], 160)
-    half = (cf[:, 7:8], cf[:, 6:7])
+    ms(T.Zr[:], 0.0, ["Zr"], 128)
+    I32 = T.IW[:, 0:128]
+    AM = lambda x, y: T.AM[:, 256 * x + 128 * y:256 * x + 128 * y + 128]
+    AH = lambda x, y: T.AH[:, 256 * x + 128 * y:256 * x + 128 * y + 128]
+    GM = lambda x: T.GM[:, 128 * x:128 * x + 128]
+    HM = lambda x: T.HM[:, 128 * x:128 * x + 128]
+    SM = lambda x: T.SM[:, 128 * x:128 * x + 128]
+    hop = lambda x, y: ([[-32, 4], [1000, 2], [-1, 16]], -16 * x - 1000 * y)
     for x in (0, 1):
         for y in (0, 1):
-            o = 16 - 16 * (y - x)
-            ts(T["A%d%d" % (x, y)][:], T.IW[:, o:o + 128], half[x], None, A.mult, None, ["IW", "h0", "h1"], ["A%d%d" % (x, y)], 128)
-        tt(T["H%d" % x][:], T["A%d0" % x][:], T["A%d1" % x][:], A.add, ["A%d0" % x, "A%d1" % x], ["H%d" % x], 256)
-    tt(T.HH[:], T.H0[:], T.H1[:], A.add, ["H0", "H1"], ["HH"], 256)
-    cp(T.Ib[:], T.IW[:, 16:144], ["IW"], ["Ib"], 128)
-    ts(T.nIb[:], T.IW[:, 16:144], -1.0, None, A.mult, None, ["IW"], ["nIb"], 128)
-    ts(T.nI[:], T.IW[:, 16:144], -1.0, None, A.mult, None, ["IW"], ["nI"], 128)
-    ts(T.I2[:], T.IW[:, 16:144], 2.0, None, A.mult, None, ["IW"], ["I2"], 128)
+            put(AM(x, y), T.Zr[:], *hop(x, y), 1.0, ["Zr"], ["A%d%d" % (x, y)])
+    put(T.Ib[:], T.Zr[:], [[-1, 128]], 0, 1.0, ["Zr"], ["Ib"])
+    for j, m in enumerate((15, 16, 112, 96)):
+        ts(T.ri[:, j + 1:j + 2], T.ri[:, 0:1], m, None, A.bitwise_and, None, ["ri"], ["ri%d" % j])
+    cf = T.cf
+    col = lambda j: cf[:, j:j + 1]
+    cp(cf[:, 0:5], T.ri[:, 0:5], ["ri"] + ["ri%d" % j for j in range(4)], ["cf"])
+    cp_, ch, c16r, c32r = [col(j) for j in range(1, 5)]
+    cp(T.AH[:], T.AM[:], ["A00", "A01", "A10", "A11"], ["AH"], 512)
     ts(T.Z0[:], T.c16[:], c16r, 16384.0, A.is_equal, A.mult, ["c16", "cf"], ["Z0"], 128)
     ts(T.Z1[:], T.c16[:], c16r, -16384.0, A.is_equal, A.mult, ["c16", "cf"], ["Z1"], 128)
     ms(T.zc[:], -8.5 * 16384, ["zc"]); ms(T.zc[:, 32:64], 8.5 * 16384, ["zc"])
-    ts(T.O32[:], T.c32[:], c32r, None, A.is_equal, None, ["c32", "cf"], ["O32"], 128)
-    ms(T.B[:], 0.0, ["B"])
-    ts(T.B[:, 16:144:16], T.c16[:, 0:128:16], c16r, 1024.0, A.is_equal, A.mult, ["c16", "cf"], ["B"])
-    ts(T.m32[:], T.cA[:, 16:48], c31, None, A.is_equal, None, ["cA", "cf"], ["m32"])
-    ms(T.EM[:], 0.0, ["EM"])
-    for q in (0, 1):
-        ts(T.EM[:, 65 * q:65 * q + 64], T.cl[:], cf[:, 8 + q:9 + q], 2.0 ** 15, A.is_ge, A.mult, ["cl", "own0", "own1", "EM"], ["EM%d" % q])
-    ts(T.DM[:], T.c16[:, 0:128:16], cp_, None, A.add, None, ["c16", "cf"], ["DM"])
-    ts(cf[:, 12:16], T.c16[:, 0:64:16], cf[:, 10:11], -1.0, A.add, A.mult, ["c16", "dm0"], ["k40"])
-    for x in (0, 1):
-        ts(T.K8[:, 8 + x:9 + x], half[1 - x], -16384.0, 4096.5, A.mult, A.add, ["h0", "h1"], ["kh%d" % x])
-        ts(T.K8[:, 4 * x:4 * x + 4], cf[:, 12:16], T.K8[:, 8 + x:9 + x], None, A.add, None, ["k40", "kh%d" % x], ["K8%d" % x])
-    ts(T.CV[:], T.c16[:, 0:32], -1.0, cf[:, 11:12], A.mult, A.add, ["c16", "cv0"], ["CV"])
-    ts(T.TC[:, 12:14], T.c16[:, 0:32:16], cp_, -1.0, A.add, A.mult, ["c16", "cf"], ["TCb"])
-    ts(T.O32e[:], T.c32[:], c32r, 0.125, A.is_equal, A.mult, ["c32", "cf"], ["O32e"], 128)
-    ms(T.kc[:], -512.0, ["kc"])
-    for t in range(RO):
-        ts(T.TC[:, 2 * t:2 * t + 2], T.TC[:, 12:14], 1024.0 * AT[t] + 1023, None, A.add, None, ["TCb"], ["TC%d" % t])
-    ms(T.rv[:], 1.0, ["rv"]); ms(T.rv[:, 0:32:16], -BIG, ["rv"])
-    nm_ = max(512, PIECE * 256)
-    ms(T.msk[:, 0:nm_], 1.0, ["msk"], nm_ // 2); ms(T.msk[:, 0:nm_:16], 0.0, ["msk"])
-    ms(T.dl[:], 32.0, ["dl"]); ms(T.dl[:, 32:64], -32.0, ["dl"]); ms(T.dl[:, 96:128], -32.0, ["dl"])
+    ts(T.cfl[:, 0:128], T.ci[:, 0:128], -CB, None, A.add, None, ["ci0", "ci1", "ci2"], ["cfl"], 128)
+    ts(T.cfl[:, 128:132], T.ci[:, 128:132], OFF, None, A.add, None, ["ci0", "ci1", "ci2"], ["cfm"])
+    ms(T.msk[:], 1.0, ["msk"], 256); ms(T.msk[:, 0:512:16], 0.0, ["msk"])
     ms(T.Pb[:, 0:1], 0.0, ["Pb0"])
-    ts(T.cfl[:], T.ci[:], OFF, None, A.add, None, ["ci0", "ci1", "ci2"], ["cfl"], 132)
+    first = len(ops)
+    io(T.c32[:], [[32, 4], [0, 32]], 0, 0, ["c32"], 128)
+    io(T.cl[:], [[16, 2], [32, 2], [1, 16]], 0, 0, ["cl"], 64)
+    io(T.CK[:], [[0, 2], [-1, 19]], 15, 0, ["CK"], 38)
+    put(I32, T.Zr[:], [[-1, 128]], 0, 1.0, ["Zr"], ["IW"])
+    put(T.nI[:], T.Zr[:], [[-1, 128]], 0, -1.0, ["Zr"], ["nI"])
+    put(T.nIb[:], T.Zr[:], [[-1, 128]], 0, -1.0, ["Zr"], ["nIb"])
+    if "q" in PB or "p" in PB:
+        put(T.I2[:], T.Zr[:], [[-1, 128]], 0, 2.0, ["Zr"], ["I2"])
+    for x in (0, 1):
+        put(HM(x), T.Zr[:], [[-32, 4], [0, 2], [-1, 16]], -16 * x, 1.0, ["Zr"], ["H%d" % x])
+        put(SM(x), T.Zr[:], [[-32, 4], [0, 32]], -2 - x, 1.0, ["Zr"], ["S%d" % x])
+        put(SM(x), SM(x), [[-32, 4], [0, 32]], -4 - x, -BIG, ["S%d" % x], ["S%d" % x])
+        put(GM(x), AM(x, 0), hop(x, 0)[0], -16 * x - 1, -1.0, ["A%d0" % x], ["G%d" % x])
+        put(T.GM[:, 128 * x + 15:128 * x + 128:32], T.Zr[:, 0:4], [[-32, 4]], -16 * x - 15, 1.0, ["Zr", "G%d" % x], ["G%d" % x], 4)
+        put(T.GM[:, 128 * x + 19:128 * x + 128:32], T.Zr[:, 0:4], [[-32, 4]], -16 * x, 1.0, ["Zr", "G%d" % x], ["Gx%d" % x], 4)
+    ts(col(8), ch, 2.0, cp_, A.mult, A.add, ["cf"], ["own0"])
+    ts(col(9), col(8), 16.0, None, A.add, None, ["own0"], ["own1"])
+    for x in (0, 1):
+        ts(T.EMf[:, 64 * x:64 * x + 64], T.cl[:], col(8 + x), -BIG, A.subtract, A.mult, ["cl", "own0", "own1"], ["EM%d" % x])
+    ts(T.EM[:], T.EMf[:], BIG, None, A.min, None, ["EM0", "EM1"], ["EM"], 128)
+    ms(T.B[:], 0.0, ["B"])
+    ts(T.B[:, 16:144:16], T.c16[:, 0:128:16], c16r, 2048.0, A.is_equal, A.mult, ["c16", "cf"], ["B"])
+    io(T.DM[:], [[64, 2], [0, 4]], 0, 0, ["DM"], 8)
+    ms(T.CV[:], 0.0, ["CV"])
+    ts(col(17), cp_, -32.0, -16.0, A.mult, A.add, ["cf"], ["cv0"])
+    for q in (0, 1):
+        ts(T.CV[:, 19 * q + 1:19 * q + 17], T.c16[:, 16 * q:16 * q + 16], -1.0, col(17), A.mult, A.add, ["c16", "cv0", "CV"], ["CV%d" % q])
+    for t in range(RO):
+        io(T.TC[:, 2 * t:2 * t + 2], [[-16, 2]], 2048 * AT[t] - 529, 0, ["TB%d" % t], 2)
+    ts(T.TC[:, 0:2 * RO], T.TC[:, 0:2 * RO], cp_, None, A.subtract, None, ["cf"] + ["TB%d" % t for t in range(RO)], ["TC"])
+    ts(T.O32e[:], T.c32[:], c32r, 2048.0, A.is_equal, A.mult, ["c32", "cf"], ["O32e"], 128)
+    ms(T.kc[:], -1024.0, ["kc"])
+    ms(T.rv[:], 1.0, ["rv"]); ms(T.rv[:, 0:38:19], -1.0e11, ["rv"]); ms(T.rv[:, 18:38:19], M2K, ["rv"])
+    ms(T.rE[:], 1.0e9, ["rE"]); ms(T.rE[:, 0:38:19], 512.0, ["rE"])
+    io(T.dl[:], [[-64, 2], [0, 64]], 32, 0, ["dl"], 128)
+    ms(T.KR[:], 0.0, ["KR"])
+    for j, c in ((15, CB + OFF), (16, -32.0), (17, M2), (18, -M2), (19, CB + OFF)):
+        ms(T.KR[:, j:64:32], c, ["KR%d" % j])
+        ops[-1]["rd"] = ["KR"]
+    tr(T.KH[:], T.KR[:], ["KR%d" % j for j in range(15, 20)], ["KH"])
+    io(T.SP[:, 0:128], [[0, 128]], 0, 0, ["SP"], 128)
+    ms(T.SP[:, 130:132], 0.0, ["SP2"])
+    ts(T.SP[:, 128:130], cf[:, 8:10], 0.5, None, A.add, None, ["own0", "own1"], ["SP1"])
+    ms(T.km[:], -M4, ["km"], 256)
+    ms(T.k1[:], 1.0, ["k1"], 256)
+    later(first, CONB)
+    POFF = [0.0 if PB[4 * f] in "gG" else OFF for f in (0, 1)]
     AK = ["A00", "A01", "A10", "A11"]
 
     def phase_setup(f):
@@ -180,40 +213,50 @@ def build(T, dst_addr, emask, nen):
         ps = [T["ps%d%d" % (f, b)] for b in range(4)]
         bk = ["bk%d%d" % (f, b) for b in range(4)]
         W = B("W")
-        ms(B("V")[:, 0:PAD], 0.0, [k("V")])
-        ms(B("U")[:, 512:544], 0.0, [k("Up")])
-        ms(B("unx")[:], 0.0, [k("unx")], 256)
-        ms(B("ex")[:, 64:65], 0.0, [k("exp")])
+        ms(B("V")[:, 0:PAD], 0.0, [k("V")], PAD // 2)
         for j in (0, 1):
             for h in (0, 1):
                 for q in (0, 1):
-                    mm(ps[2][:, 32 * j + 16 * h:32 * j + 16 * h + 16], T["A%d%d" % (f, q)][:], T.cfl[:, 64 * j + 2 * h + q:64 * j + 64:4], q == 0, q == 1,
+                    mm(ps[2][:, 32 * j + 16 * h:32 * j + 16 * h + 16], AM(f, q), T.cfl[:, 64 * j + 2 * h + q:64 * j + 64:4], q == 0, q == 1,
                        ["cfl"] + AK, bk[2], 16, True)
         for h in (0, 1):
-            mm(ps[2][:, 64:66], T["A%d%d" % (f, h)][:], T.cfl[:, 128 + 2 * h:130 + 2 * h], h == 0, h == 1, ["cfl"] + AK, bk[2], 2, True)
+            mm(ps[2][:, 64:66], AM(f, h), T.cfl[:, 128 + 2 * h:130 + 2 * h], h == 0, h == 1, ["cfm"] + AK, bk[2], 2, True)
         tr(W[:, 512:576], ps[2][:, 0:64], [], [k("in0")], 64, bk[2])
         cp(W[:, 576:578], ps[2][:, 64:66], [], [k("in0a")], 64, bk[2])
         q_ = B("q")
-        ts(q_[:, 8:10], W[:, 576:578], M2, -M2, A.add, A.add, [k("in0a")], [k("r")])
-        tt(q_[:, 10:12], q_[:, 8:10], W[:, 576:578], A.subtract, [k("r"), k("in0a")], [k("r1")])
-        tt(W[:, 578:580], q_[:, 10:12], q_[:, 8:10], A.add, [k("r"), k("r1")], [k("in0b")])
-        ts(q_[:, 0:2], T.TC[:, 0:2], -512.0, None, A.add, None, ["TC0"], [k("T")])
+        ts(q_[:, 4:6], W[:, 576:578], M2, -M2 - 32, A.add, A.add, [k("in0a")], [k("r0")])
+        for q in (0, 1):
+            ts(W[:, 578 + q:579 + q], q_[:, 4 + q:5 + q], 2.0, W[:, 576 + q:577 + q], A.mult, A.subtract, [k("r0"), k("in0a")], [k("in0b%d" % q)])
+        first = len(ops)
+        ms(B("U")[:, 512:544], 0.0, [k("Up")])
+        io(B("unx")[:], [[0, 512]], 0, 0, [k("unx")], 512)
+        io(B("D")[:], [[0, 164 * RO]], 0, 0, ["Dz%d%d" % (t, f) for t in range(RO)], 164 * RO)
+        later(first, CONB)
         P = B("P")
         first = len(ops)
         for i in range(4):
             ev, od = P[:, 1024 * i:1024 * i + 1024:2], P[:, 1024 * i + 1:1024 * i + 1024:2]
             y = T.y1[:, 512 * i:512 * i + 512]
             b = 3 * (i % 2)
-            ts(ev, B("gi")[:, 512 * i:512 * i + 512], OFF, None, A.add, None, ["ld%s%d%d" % ("gh"[i // 2], f, j) for j in range(8)], [k("Pe%d" % i)], 512)
             how = PB[4 * f + i]
+            ld = ["ld%s%d%d" % ("gh"[i // 2], f, j) for j in range(8)]
+            if how in "gG":
+                move(ev, B("gi")[:, 512 * i:512 * i + 512], 512, ld, [k("Pe%d" % i)])
+                act(y, ev, [k("Pe%d" % i)], ["y%d" % i], 512, M4, 1.9998)
+                mm(ps[b][:], I32, y, True, False, ["IW", "y%d" % i], bk[b], 512, True)
+                mm(ps[b][:], T.Ib[:], T.km[:], False, False, ["Ib", "km"], bk[b], 512)
+                mm(ps[b][:], T.Ib[:], T.k1[:], False, False, ["Ib", "k1"], bk[b], 512)
+                mm(ps[b][:], T.nI[:], ev, False, True, ["nI", k("Pe%d" % i)], bk[b], 512, True)
+                if how == "G":
+                    act(od, ps[b][:], [], [k("Po%d" % i)], 512, 0.0, 1.0, bk[b])
+                else:
+                    cp(od, ps[b][:], [], [k("Po%d" % i)], 512, bk[b])
+                continue
+            ts(ev, B("gi")[:, 512 * i:512 * i + 512], POFF[f], None, A.add, None, ld, [k("Pe%d" % i)], 512)
             if how == "a":
                 act(y, ev, [k("Pe%d" % i)], ["y%d" % i], 512, M4, 2.0)
                 act(ps[b][:], y, ["y%d" % i], [], 512, -M4, 1.0, bk[b])
                 tt(od, ps[b][:], ev, A.subtract, [k("Pe%d" % i)], [k("Po%d" % i)], 512, bk[b])
-            elif how == "v":
-                ts(y, ev, 2.0, M4, A.mult, A.add, [k("Pe%d" % i)], ["y%d" % i], 512)
-                ts(ps[b][:], y, -M4, None, A.add, None, ["y%d" % i], [k("z%d" % b)], 512, bk[b])
-                tt(od, ps[b][:], ev, A.subtract, [k("Pe%d" % i), k("z%d" % b)], [k("Po%d" % i)], 512, bk[b])
             else:
                 ts(y, ev, M2, -M2, A.add, A.add, [k("Pe%d" % i)], ["y%d" % i], 512)
                 mm(ps[b][:], T.I2[:], y, True, False, ["I2", "y%d" % i], bk[b], 512, True)
@@ -222,60 +265,78 @@ def build(T, dst_addr, emask, nen):
                     act(od, ps[b][:], [], [k("Po%d" % i)], 512, 0.0, 1.0, bk[b])
                 else:
                     cp(od, ps[b][:], [], [k("Po%d" % i)], 512, bk[b])
-        for o in ops[first:]:
-            o["bulk"] = f
+        later(first, f * P1B)
 
     def phase(t, f):
         B = lambda n: T[n + str(f)]
         k = lambda n: n + str(f)
         ps = [T["ps%d%d" % (f, b)] for b in range(4)]
         bk = ["bk%d%d" % (f, b) for b in range(4)]
-        w0, s0 = 584 * t, 72 * t
-        W, SB, q_ = B("W"), B("SB"), B("q")
-        Wc = lambda a, b, c=1: W[:, w0 + a:w0 + b:c] if c > 1 else W[:, w0 + a:w0 + b]
+        w0, s0, d0 = 584 * t, 64 * t, 164 * t
+        W, SB, D, q_, LT, Y = B("W"), B("SB"), B("D"), B("q"), B("LT"), B("Y")
+        Wc = lambda a, b: W[:, w0 + a:w0 + b]
         Sc = lambda a, b: SB[:, s0 + a:s0 + b]
-        INL = [k("in0a"), k("in0b")] if t == 0 else [k("inb%d_" % t)]
-        IN = INL + [k("in0") if t == 0 else k("ina%d_" % t)]
+        Dc = lambda a, b, c=1: D[:, d0 + a:d0 + b:c] if c > 1 else D[:, d0 + a:d0 + b]
+        INL = [k("in0a"), k("in0b0"), k("in0b1")] if t == 0 else [k("inb%d_" % t)]
+        INC = [k("in0") if t == 0 else k("ina%d_" % t)]
+        came = Wc(512, 576) if t == 0 else B("Wa")[:, s0:s0 + 64]
         VK = [k("V")] + (["ldv%d%d" % (f, j) for j in range(8)] if t == 0 else [])
         PK = [k("P%s%d" % (a, i)) for a in "eo" for i in range(4)]
         Vw = B("V")[:, 0:NV]
         sb = lambda n: "%s%d%d" % (n, t, f)
 
-        def send(part, a, b, rd):
+        def send(part, dst, src, rd):
             if t + 1 < RO:
                 sem = "arr%s%d%d" % (part, t + 1, f)
-                op("G", lambda e: e.remote_dma(W[:, w0 + 584 + 512 + a:w0 + 584 + 512 + b], Sc(a, b), T.sem[sem], T.sem.sent, dst_addr[1], dst_addr[0], emask),
-                   rd, [sb("gone" + part)], 300, None, "sent", 0)
-                op("N", None, [sb("gone" + part)], [k("in%s%d_" % (part, t + 1))], NET, None, sem, nen)
+                op("G", lambda e: e.remote_dma(dst, src, T.sem[sem], T.sem.sent, dst_addr[1], dst_addr[0], emask),
+                   rd, [sb("gone" + part)], 0, None, "sent", 0, fx=300.0)
+                op("N", None, [sb("gone" + part)], [k("in%s%d_" % (part, t + 1))], 0, None, sem, nen)
 
         ts(B("Lu")[:], Wc(576, 580), 0.5, None, A.add, None, INL, [k("Lu")])
-        cp(B("g1")[:], Vw.indirect(B("Lu")[:, 0:4]), VK + [k("Lu")], [k("g1")], 50 + 64 * GA)
-        tt(B("less")[:], B("g1")[:, 0:32], B("g1")[:, 32:64], A.is_lt, [k("g1")], [k("less")])
+        cp(B("g1")[:], B("V")[:, 64:NV].indirect(B("Lu")[:, 2:4]), VK + [k("Lu")], [k("g1")], gn=32)
+        tt(B("less")[:], Vw.indirect(B("Lu")[:, 0:2]), B("g1")[:], A.is_lt, VK + [k("Lu"), k("g1")], [k("less")], gn=32)
         for x in (0, 1):
             o = ps[2][:, 300 + 32 * x:332 + 32 * x]
             mm(o, T.Ib[:], T.zc[:, 32 * x:32 * x + 32], True, False, ["Ib", "zc"], bk[2])
             mm(o, T["Z%d" % x][:], B("less")[:], False, True, ["Z0", "Z1", k("less")], bk[2])
-        tt(B("X")[:], ps[2][:, 300:364], Wc(512, 576), A.min, IN, [k("XX")], 64, bk[2])
+        tt(B("X")[:], ps[2][:, 300:364], came, A.min, INC, [k("XX")], 64, bk[2])
         tt(Sc(0, 32), B("X")[:, 0:32], B("X")[:, 32:64], A.max, [k("XX")], [sb("c")])
         for x in (0, 1):
             for y in (0, 1):
-                mm(ps[2][:, 32 + x:64:2], T["A%d%d" % (x, y)][:], Sc(16 * y, 16 * y + 16), y == 0, y == 1, [sb("c")] + AK, bk[2], 16, True)
-        ts(B("Lc")[:], ps[2][:, 32:64], -OFF, None, A.add, None, [], [k("Lc")], 64, bk[2])
+                mm(ps[2][:, 32 + x:64:2], AH(x, y), Sc(16 * y, 16 * y + 16), y == 0, y == 1, [sb("c"), "AH"], bk[2], 16)
+        ts(B("Lc")[:], ps[2][:, 32:64], CB, None, A.add, None, [], [k("Lc")], 64, bk[2])
+        if t:
+            move(Wc(512, 544), B("Wa")[:, s0:s0 + 32], 32, INC + [k("Lc")], [sb("Dw")])
+            ops[-1]["bulk"] = 1
         for u, (a, b) in enumerate(zip([0] + IMG, IMG + [32])):
-            gat(B("I")[:, 16 * a:16 * b], B("P")[:, 0:4096].indirect(B("Lc")[:, a:b]), PK + [k("Lc")], [k("I%d" % u)], 16 * (b - a))
-            tr(Wc(16 * a, 16 * b), B("I")[:, 16 * a:16 * b], [k("I%d" % u)], [sb("O%d" % u)], 16 * (b - a))
-            ts(B("Ou")[:, 16 * a:16 * b], Wc(16 * a, 16 * b), 0.5, None, A.add, None, [sb("O%d" % u)], [k("Ou_%d_" % z) for z in range(a, b)], 16 * (b - a))
+            src = B("P")[:, 0:4096].indirect(B("Lc")[:, a:b])
+            ou = [k("Ou_%d_" % z) for z in range(a, b)]
+            n = 16 * (b - a)
+            if (t, f) in IMG_ACT:
+                gat(T.I[:, 16 * a:16 * b], src, PK + [k("Lc")], ["I%d" % u], n, -POFF[f] - CB)
+                tr(Wc(16 * a, 16 * b), T.I[:, 16 * a:16 * b], ["I%d" % u], [sb("O%d" % u)], n)
+                ts(B("Ou")[:, 16 * a:16 * b], Wc(16 * a, 16 * b), CB + PAD, None, A.add, None, [sb("O%d" % u)], ou, n)
+            else:
+                ts(T.Ih[:, 16 * a:16 * b], src, -POFF[f] - CB, None, A.add, None, PK + [k("Lc")], ["Ih%d" % u], gn=n)
+                tr(T.Wh[:, 16 * a:16 * b], T.Ih[:, 16 * a:16 * b], ["Ih%d" % u], ["Wh%d" % u], n // 2)
+                ts(B("Ou")[:, 16 * a:16 * b], T.Wh[:, 16 * a:16 * b], CB + PAD, None, A.add, None, ["Wh%d" % u], ou, n // 2)
+                if u:
+                    later(len(ops) - 3, IMGB[u - 1])
+                move(Wc(16 * a, 16 * b), T.Wh[:, 16 * a:16 * b], n, ["Wh%d" % u], [sb("O%d" % u)])
+                ops[-1]["bulk"] = 1
         a0 = held = 0
         UK = []
         for ci, n in enumerate(CHUNKS):
             nv = VSHARE.get((t, f, ci), 0)
             lk = lambda nm, a, b: [k("%s_%d_" % (nm, x)) for x in range(a, b)]
             ou = lk("Ou", a0, a0 + n)
-            gat(B("w")[:, 256 * a0:256 * (a0 + n - nv)], Vw.indirect(B("Ou")[:, 16 * a0:16 * (a0 + n - nv)]), VK + ou, lk("w", a0, a0 + n - nv), 256 * (n - nv))
-            ops[-1]["bulk"] = 1
-            ops[-1]["bk"] = "gathers"
+            if nv < n:
+                gat(B("w")[:, 256 * a0:256 * (a0 + n - nv)], Vw.indirect(B("Ou")[:, 16 * a0:16 * (a0 + n - nv)]), VK + ou, lk("w", a0, a0 + n - nv), 256 * (n - nv))
+                ops[-1]["bulk"] = 1
+                ops[-1]["bk"] = "gathers"
             if nv:
-                cp(B("w")[:, 256 * (a0 + n - nv):256 * (a0 + n)], Vw.indirect(B("Ou")[:, 16 * (a0 + n - nv):16 * (a0 + n)]), VK + ou, lk("w", a0 + n - nv, a0 + n), 50 + 256 * nv * GA)
+                cp(B("w")[:, 256 * (a0 + n - nv):256 * (a0 + n)], Vw.indirect(B("Ou")[:, 16 * (a0 + n - nv):16 * (a0 + n)]), VK + ou, lk("w", a0 + n - nv, a0 + n), gn=256 * nv)
+                ops[-1]["bulk"] = 1
             mx = T.Mx[:, 16 * a0:16 * (a0 + n)]
             mk_ = ["Mx_%d" % z for z in range(a0, a0 + n)]
             short = ci >= len(CHUNKS) - SHORT
@@ -316,94 +377,97 @@ def build(T, dst_addr, emask, nen):
             mm(dps, T.nIb[:], T.s[:, 256 * a0 + 15:256 * (a0 + n):16], False, True, ["s_%d" % z for z in range(a0, a0 + n)] + ["nIb"], bk[db], 16 * n)
             uk = k("U%d" % ci)
             UK.append(uk)
-            if ci < UNIT_ACT:
+            if ci < UNIT_ACT.get((t, f), UNIT_DEF):
                 act(B("U")[:, 16 * a0:16 * (a0 + n)], dps, [], [uk], 16 * n, -256.0 * (MT[t] + 0.5), 256.0, bk[db], F.Sigmoid)
             else:
                 ts(B("U")[:, 16 * a0:16 * (a0 + n)], dps, MT[t] + 0.5, None, A.is_gt, None, [], [uk], 16 * n, bk[db])
             for p in range(a0 // 2, (a0 + n) // 2):
                 if p == 0:
-                    mm(ps[1][:, 0:32], T.Ib[:], T.CV[:], True, False, ["Ib", "CV"], bk[1])
-                mm(ps[1][:, 0:32], T.B[:, 16 - p:144 - p], B("U")[:, 32 * p:32 * p + 32], False, p == 15, ["B", uk], bk[1])
+                    mm(ps[1][:, 0:38], T.Ib[:], T.CV[:], True, False, ["Ib", "CV0", "CV1"], bk[1])
+                    mm(ps[1][:, 0:38:19], I32, T.TC[:, 2 * t:2 * t + 2], False, False, ["IW", "TC"], bk[1], 2, True)
+                    for q in range(2 if t else 0):
+                        for x in (0, 1):
+                            mm(ps[1][:, 19 * q:19 * q + 1], T.O32e[:], Dc(x - 28, x - 27), False, False, ["O32e", "pro%d%d" % (t - 1, f)], bk[1], 1, True)
+                        mm(ps[1][:, 19 * q:19 * q + 1], T.nI[:], q_[:, 2:3], False, False, ["nI", k("a1")], bk[1], 1, True)
+                for q in (0, 1):
+                    mm(ps[1][:, 19 * q + 1:19 * q + 17], T.B[:, 16 - p:144 - p], B("U")[:, 32 * p + 16 * q:32 * p + 16 * q + 16], False, p == 15 and q == 1, ["B", uk], bk[1])
             a0 += n
-        en = B("en")
-        scan(B("ev")[:], T.rv[:], ps[1][:, 0:32], A.add, A.max, ["rv"], [k("ev")], 64, bk[1])
-        tt(en[:, 0:2], B("ev")[:, 15:32:16], q_[:, 0:2], A.max, [k("ev"), k("T")], [k("en")])
-        ts(en[:, 2:4], en[:, 0:2], 1023, None, A.bitwise_and, None, [k("en")], [k("enx")])
-        ts(B("J")[:], en[:, 2:4], -1.0, 1023.0, A.mult, A.add, [k("enx")], [k("J")])
-        pro = B("pro")
-        ts(pro[:], en[:, 2:4], 511.5, 8192.0, A.is_ge, A.mult, [k("enx")], [k("pro")])
-        OK = [sb("O%d" % u) for u in range(len(IMG) + 1)] + [k("J")] + IN
-        ts(B("Cu")[:], Wc(0, 544).indirect(B("J")[:, 0:2]), 0.5, None, A.add, None, OK, [k("Cu")], 100)
-        cp(B("unx")[:, 0:512:16], B("U")[:, 0:544].indirect(B("J")[:, 0:2]), UK + [k("Up"), k("J")], [k("unx")], 100)
-        cp(Sc(32, 64), Wc(0, 544).indirect(B("J")[:, 0:2]), OK, [sb("C")], 100)
-        send("a", 0, 64, [sb("c"), sb("C")])
-        scan(B("unb")[:], T.msk[:, 0:512], B("unx")[:], A.mult, A.add, ["msk", k("unx")], [k("unb")], 256)
-        for h in (0, 1):
-            for q in (0, 1):
-                mm(ps[2][:, 64 + 16 * h:80 + 16 * h], T["A%d%d" % (h, q)][:], Sc(32 + 16 * q, 48 + 16 * q), q == 0, q == 1, [sb("C")] + AK, bk[2], 16, True)
-        tr(B("LT")[:], ps[2][:, 64:96], [], [k("LT")], 64, bk[2])
+        ev = B("ev")
+        scan(ev[:], T.rv[:], ps[1][:, 0:38], A.add, A.max, ["rv"], [k("ev")], 64, bk[1])
         for q in (0, 1):
-            ts(B("L8")[:, 16 * q:16 * q + 16], B("LT")[:, 16 * q:16 * q + 16], Wc(576 + q, 577 + q), pro[:, q:q + 1], A.subtract, A.mult, [k("LT"), k("pro")] + IN, [k("L8%d" % q)])
-            ts(B("L8")[:, 16 * q:16 * q + 16], B("L8")[:, 16 * q:16 * q + 16], 1.0 / 8192, Wc(576 + q, 577 + q), A.mult, A.add, [k("L8%d" % q)] + IN, [k("L8%d" % q)])
-        mm(ps[1][:, 32:64], T.Ib[:], T.CK[:], True, False, ["Ib", "CK"], bk[1])
-        for a, b in zip([0] + SUMS, SUMS + [16]):
-            for q in (0, 1):
-                tt(B("pr")[:, 32 * a + q:32 * b:2], Vw.indirect(B("Cu")[:, 16 * q + a:16 * q + b]), B("unb")[:, 256 * q + 16 * a:256 * q + 16 * b], A.mult,
-                   VK + [k("Cu"), k("unb")], [k("pr%d_%d_" % (q, p)) for p in range(a, b)], 50 + 16 * (b - a) * GA)
-            for p in range(a, b):
-                mm(ps[1][:, 32:64], T.B[:, 16 - p:144 - p], B("pr")[:, 32 * p:32 * p + 32], False, p == 15, ["B", k("pr0_%d_" % p), k("pr1_%d_" % p)], bk[1])
+            ts(B("J")[:, q:q + 1], ev[:, 19 * q + 18:19 * q + 19], -M2K, ev[:, 19 * q + 17:19 * q + 18], A.add, A.subtract, [k("ev")], [k("J%d" % q)])
+        JK = [k("J0"), k("J1")]
+        OK = [sb("O%d" % u) for u in range(len(IMG) + 1)] + JK + ([sb("Dw")] if t else INC)
+        cp(B("unx")[:, 0:512:16], B("U")[:, 0:544].indirect(B("J")[:, 0:2]), UK + [k("Up")] + JK, [k("unx")], gn=32)
+        cp(Sc(32, 64), Wc(0, 544).indirect(B("J")[:, 0:2]), OK, [sb("C")], gn=32)
+        ts(Dc(136, 138), B("J")[:], 511.5, None, A.is_lt, None, JK + [sb("Dz")], [sb("pro")])
+        send("a", B("Wa")[:, s0 + 64:s0 + 128], Sc(0, 64), [sb("c"), sb("C")])
+        ts(B("Cu")[:], Sc(32, 64), CB + PAD, None, A.add, None, [sb("C")], [k("Cu")])
+        scan(B("unb")[:], T.msk[:, 0:512], B("unx")[:], A.mult, A.add, ["msk", k("unx")], [k("unb0"), k("unb1")], 256)
+        mm(ps[2][:, 64:128], I32, T.KH[:], True, False, ["IW", "KH"], bk[2], 64, True)
         for q in (0, 1):
-            V(lambda e, q=q: e.tensor_reduce(B("sm")[:, q:q + 1], ps[1][:, 32 + q:64:2], AxisListType.X, A.max), [], [k("sm%d" % q)], 64, bk[1])
+            for h in (0, 1):
+                mm(ps[2][:, 64 + 32 * q + 16 * h:80 + 32 * q + 16 * h], GM(h), Sc(32 + 16 * q, 48 + 16 * q), False, h + q == 2, [sb("C"), "Gx0", "Gx1"], bk[2], 16)
+        tr(LT[:], ps[2][:, 64:128], [], [k("LT")], 64, bk[2])
+        mm(ps[2][:, 264:266], I32, Wc(576, 578), True, False, ["IW"] + INL, bk[2], 2, True)
+        mm(ps[2][:, 264:266], T.nI[:], LT[:, 19:64:32], False, True, ["nI", k("LT")], bk[2], 2, True)
+        cd = ps[1][:, 64:102]
+        mm(cd, T.Ib[:], T.CK[:], True, False, ["Ib", "CK"], bk[1])
         for q in (0, 1):
-            ts(B("eq")[:, 16 * q:16 * q + 16], ps[1][:, 32 + q:64:2], B("sm")[:, q:q + 1], None, A.is_equal, None, [k("sm%d" % q)], [k("eq%d" % q)], 64, bk[1])
-        tt(B("mu")[:], B("eq")[:], B("L8")[:], A.mult, [k("eq0"), k("eq1"), k("L80"), k("L81")], [k("mu")])
+            tt(B("pr")[:, 256 * q:256 * q + 256], Vw.indirect(B("Cu")[:, 16 * q:16 * q + 16]), B("unb")[:, 256 * q:256 * q + 256], A.mult,
+               VK + [k("Cu"), k("unb%d" % q)], [k("pr%d" % q)], gn=256)
+            for p in range(16):
+                mm(ps[1][:, 64 + 19 * q:80 + 19 * q], T.B[:, 16 - p:144 - p], B("pr")[:, 256 * q + 16 * p:256 * q + 16 * p + 16], False, p + q == 16, ["B", k("pr%d" % q)], bk[1])
+        scan(B("Eb")[:], T.rE[:], cd, A.min, A.max, ["rE"], [k("Eb")], 64, bk[1], 1.0e9)
+        tt(B("nr")[:], cd, B("Eb")[:], A.is_lt, [k("Eb")], [k("nr")], 64, bk[1])
         for q in (0, 1):
-            red(Sc(64 + q, 65 + q), B("mu")[:, 16 * q:16 * q + 16], A.add, [k("mu")], [sb("l%d" % q)])
+            scan(Dc(98 + q, 136, 2), B("nr")[:, 19 * q:19 * q + 19], LT[:, 32 * q:32 * q + 19], A.mult, A.add, [k("nr"), k("LT"), sb("Dz")], [sb("l%d" % q)], 64, bk[2], ps[2][:, 264 + q:265 + q])
         LK = [sb("l0"), sb("l1")]
-        ts(q_[:, 8:10], Sc(64, 66), M2, -M2, A.add, A.add, LK, [k("r")])
         for q in (0, 1):
-            ts(B("ex")[:, 32 * q:32 * q + 32], T.m32[:], Sc(64 + q, 65 + q), pro[:, q:q + 1], A.mult, A.mult, ["m32", sb("l%d" % q), k("pro")], [k("ex%d" % q)])
-        tt(q_[:, 10:12], q_[:, 8:10], Sc(64, 66), A.subtract, [k("r")] + LK, [k("r1")])
-        tt(Sc(66, 68), q_[:, 10:12], q_[:, 8:10], A.add, [k("r"), k("r1")], [sb("lp")])
-        send("b", 64, 68, [sb("lp")] + LK)
-        mm(ps[3][:, 0:65], T.O32[:], B("ex")[:], True, True, ["O32", k("ex0"), k("ex1"), k("exp")], bk[3], 65, True)
+            ts(Dc(130 + q, 131 + q), Dc(134 + q, 135 + q), 2.0, Dc(128 + q, 129 + q), A.mult, A.subtract, [sb("l%d" % q)], [sb("lp%d" % q)])
+        PKK = [sb("lp0"), sb("lp1")]
+        send("b", W[:, w0 + 584 + 576:w0 + 584 + 580], Dc(128, 132), PKK + LK)
+        tr(B("TT")[:], Dc(132, 164), LK + [sb("pro"), sb("Dz")], [k("TT")])
+        mm(ps[3][:, 0:128], T.Ib[:], T.EM[:], True, False, ["Ib", "EM"], bk[3], 128)
+        for q in (0, 1):
+            for x in (0, 1):
+                mm(ps[3][:, 64 * q + 32 * x:64 * q + 32 * x + 32], SM(x), B("TT")[:], False, q + x == 2, ["S0", "S1", k("TT")], bk[3], 32, True)
         mm(ps[0][:, 0:8], T.Ib[:], T.DM[:], True, False, ["Ib", "DM"], bk[0])
-        x8 = B("x8")
         for q in (0, 1):
-            ts(B("em")[:, 65 * q:65 * q + 65], T.EM[:, 65 * q:65 * q + 65], q_[:, 8 + q:9 + q], pro[:, q:q + 1], A.subtract, A.mult, ["EM", "EM0", "EM1", k("r"), k("pro")], [k("em%d" % q)], 65)
-            tt(x8[:, 4 * q:4 * q + 4], Sc(64, 68), T.K8[:, 4 * q:4 * q + 4], A.add, LK + [sb("lp"), "K80", "K81"], [k("A2%d" % q)])
+            ts(Dc(q, 128, 2), ps[3][:, 64 * q:64 * q + 64], Dc(134 + q, 135 + q), 32768.0, A.not_equal, A.mult, LK, [sb("ne%d" % q)], 64, bk[3])
         for q in (0, 1):
-            tt(B("d")[:, 65 * q:65 * q + 65], ps[3][:, 0:65], B("em")[:, 65 * q:65 * q + 65], A.add, [k("em%d" % q)], [k("d%d" % q)], 65, bk[3])
-        for q in (0, 1):
-            red(q_[:, 14 + q:15 + q], B("d")[:, 65 * q:65 * q + 65], A.min, [k("d%d" % q)], [k("mn%d" % q)], True)
-            ts(x8[:, 8 + q:16:2], x8[:, q:8:2], q_[:, 14 + q:15 + q], 4096.0, A.min, A.max, [k("mn%d" % q), k("A20"), k("A21")], [k("X%d" % q)])
-        mm(ps[0][:, 0:8], T.HH[:], x8[:, 8:16], False, True, ["HH", k("X0"), k("X1")], bk[0], 8, True)
-        ts(B("T8")[:], ps[0][:, 0:8], -8192.0, None, A.add, None, [], [k("T8")], 64, bk[0])
-        tt(B("up")[:], Vw.indirect(B("T8")[:, 0:8]), T.dl[:], A.add, VK + [k("T8"), "dl"], [k("up")], 50 + 128 * GA)
-        ts(B("nw")[:], B("up")[:], 0.0, 255.0, A.max, A.min, [k("up")], [k("nw")])
-        cp(Vw.indirect(B("T8")[:, 0:8]), B("nw")[:], VK[1:] + [k("nw"), k("T8")], [k("V")], 50 + 128 * SCAT)
+            scan(Y[:, q:132:2], T.SP[:, q:132:2], Dc(q, 132, 2), A.max, A.min, ["SP", "SP1", "SP2", sb("ne%d" % q), sb("lp%d" % q)], [k("Y%d" % q)], 66, None, 32768.0)
+        for x in (0, 1):
+            mm(ps[0][:, x:8:2], HM(x), Y[:, 128:132], False, x == 1, ["H0", "H1", k("Y0"), k("Y1")], bk[0], 4, True)
+        ts(B("T8")[:], ps[0][:, 0:8], 0.5, None, A.add, None, [], [k("T8")], 64, bk[0])
+        ts(B("up")[:, 0:64], Vw.indirect(B("T8")[:, 0:4]), 223.0, None, A.min, None, VK + [k("T8")], [k("up")], gn=64)
+        ts(B("up")[:, 64:128], Vw.indirect(B("T8")[:, 4:8]), 32.0, None, A.max, None, VK + [k("T8")], [k("dn")], gn=64)
+        V(lambda e: e.tensor_tensor(Vw.indirect(B("T8")[:, 0:8]), B("up")[:], T.dl[:], A.add), VK[1:] + [k("up"), k("dn"), k("T8"), "dl"], [k("V")], sn=128)
         if t + 1 < RO:
-            mm(ps[2][:, 96:97], T.Ib[:], T.kc[:, 0:1], True, False, ["Ib", "kc"], bk[2])
+            mm(ps[2][:, 128:129], T.Ib[:], T.kc[:, 0:1], True, False, ["Ib", "kc"], bk[2])
             for q in (0, 1):
-                mm(ps[2][:, 96:97], T.O32e[:], pro[:, q:q + 1], False, q == 1, ["O32e", k("pro")], bk[2], 1, True)
-            ts(q_[:, 24:25], ps[2][:, 96:97], M2K, -M2K, A.add, A.add, [], [k("a1")], 64, bk[2])
-            ts(q_[:, 0:2], T.TC[:, 2 * t + 2:2 * t + 4], ps[2][:, 96:97], q_[:, 24:25], A.add, A.subtract, ["TC%d" % (t + 1), k("a1")], [k("T")], 64, bk[2])
+                mm(ps[2][:, 128:129], T.O32e[:], Dc(136 + q, 137 + q), False, q == 1, ["O32e", sb("pro")], bk[2], 1, True)
+            ts(q_[:, 2:3], ps[2][:, 128:129], M4K, -M4K, A.add, A.add, [], [k("a1")], 64, bk[2])
         else:
-            tr(B("X")[:], Sc(0, 64), [sb("c"), sb("C")], [k("XX")])
+            tr(B("Xh")[:], Sc(0, 64), [sb("c"), sb("C")], [k("Xh")])
             for j in (0, 1):
                 for h in (0, 1):
                     for q in (0, 1):
-                        mm(ps[2][:, 128 + 64 * j + 2 * h + q:192 + 64 * j:4], T["A%d%d" % (q, f)][:], B("X")[:, 32 * j + 16 * h:32 * j + 16 * h + 16], True, True,
-                           [k("XX")] + AK, bk[2], 16, True)
-            for h in (0, 1):
-                mm(ps[2][:, 256 + 2 * h:258 + 2 * h], T["A%d%d" % (h, f)][:], Sc(64, 66), True, True, LK + AK, bk[2], 2, True)
+                        mm(ps[2][:, 128 + 64 * j + 2 * h + q:192 + 64 * j:4], AH(q, f), B("Xh")[:, 32 * j + 16 * h:32 * j + 16 * h + 16], True, True,
+                           [k("Xh"), "AH"], bk[2], 16)
             if f == 0:
-                ts(T.finA[:], ps[2][:, 128:260], -OFF, None, A.add, None, [], ["finA"], 132, bk[2])
+                ts(T.finA[:, 0:128], ps[2][:, 128:256], CB, None, A.add, None, [], ["finA"], 128, bk[2])
             else:
-                tt(T.fin[:], ps[2][:, 128:260], T.finA[:], A.add, ["finA"], ["fin"], 132, bk[2])
+                tt(T.fin[:, 0:128], ps[2][:, 128:256], T.finA[:, 0:128], A.add, ["finA"], ["fin"], 128, bk[2])
                 dma("S", T.yd[:], T.fin[:, 0:64], ["fin"], [], "sto", 2000)
                 dma("S", T.yc[:], T.fin[:, 64:128], ["fin"], [], "sto", 2000)
-                dma("S", T.yl[:], T.fin[:, 128:132], ["fin"], [], "sto", 2000)
+            for h in (0, 1):
+                mm(ps[2][:, 256 + 2 * h:258 + 2 * h], AM(h, f), Dc(128, 130), True, True, LK + AK, bk[2], 2, True)
+            if f == 0:
+                ts(T.finA[:, 128:132], ps[2][:, 256:260], -OFF, None, A.add, None, [], ["finB"], 64, bk[2])
+            else:
+                tt(T.fin[:, 128:132], ps[2][:, 256:260], T.finA[:, 128:132], A.add, ["finB"], ["finl"], 64, bk[2])
+                dma("S", T.yl[:], T.fin[:, 128:132], ["finl"], [], "sto", 2000)
             for j in range(4):
                 r0 = 32 * j + 16 * f
                 dma("A" if f == 1 and j % 2 else "S", T.yv[r0:r0 + 16, :], B("V")[r0:r0 + 16, PAD:], [k("V")], [], "stv%d" % f, 3000)
@@ -417,10 +481,7 @@ def build(T, dst_addr, emask, nen):
             late = [o for o in ops[first:] if o["e"] == "V" and not o.get("bulk")]
             for o in late[DEFER:]:
                 o["bulk"] = 1.5
-        second = len(ops)
         phase(t, 1)
-        for i in range(first, len(ops)):
-            ops[i]["k"] = i - (first if i < second else second)
     return ops
 
 
@@ -448,6 +509,10 @@ def link(ops):
         o["hard"], o["soft"] = hard, soft - hard
 
 
+def kind(o):
+    return o["wr"][0].rstrip("0123456789_") if o["wr"] else ""
+
+
 def schedule(ops):
     n = len(ops)
     succ = [[] for _ in ops]
@@ -458,8 +523,6 @@ def schedule(ops):
     for i in range(n - 1, -1, -1):
         o = ops[i]
         pri[i] = o["c"] + o.get("lat", 0) + max([pri[j] + ((OWN if ops[j]["e"] == o["e"] else LAT) if i in ops[j]["hard"] else 0) for j in succ[i]] + [0])
-    for i, o in enumerate(ops):
-        pri[i] += NUDGE * (((o.get("k", 0) + 1) * (2 * SEED + 1) * 2654435761 >> 8) % 1000 / 1000.0)
     left = [len(o["hard"] | o["soft"]) for o in ops]
     rdy = [0.0] * n
     free = {e: 0.0 for e in "VAPGSN"}
@@ -480,7 +543,7 @@ def schedule(ops):
         t0, e = best
         i = max((i for i in cand[e] if rdy[i] <= t0), key=lambda i: pri[i] - BULK * ops[i].get("bulk", 0))
         if ops[i].get("bulk"):
-            soon = [j for j in cand[e] if rdy[j] <= t0 + LOOK and not ops[j].get("bulk")]
+            soon = [j for j in cand[e] if rdy[j] <= t0 + WAIT.get(kind(ops[j]), LOOK) and not ops[j].get("bulk")]
             if soon:
                 i = min(soon, key=lambda j: rdy[j])
         t0 = max(t0, rdy[i])

from concourse.mybir import AluOpType as A, AxisListType, ActivationFunctionType as F

RO = 6
MT = [16, 12, 20, 14, 24, 10]
AT = [8, 10, 7, 9, 6, 11]
PAD = 144
NV = PAD + 4096
OFF = PAD - 0.5
CB = 2048.0
M2, M4, M2K, M4K = 1.5 * 2 ** 24, 1.5 * 2 ** 25, 1.5 * 2 ** 34, 1.5 * 2 ** 35
BIG = 8192.0
CHUNKS = [4, 4, 4, 4, 4, 4, 4, 2, 2]
PIECE = 2
SHORT = 1
IMG = [8]
IMGB = [0, 0, 0]
JOIN = (0, 1, 3, 4)
VSHARE = {}
UNIT_ACT = {}
UNIT_DEF = 6
IMG_ACT = set()
PB = "aaaaqqqq"
CONB = 0.5
P1B = 1
DEFER = 14
WAIT = {}
LOOK, BULK = 40.0, 20000.0

IMG_ACT, WAIT, SHORT, JOIN, IMGB, DEFER, P1B, CONB, PB = {(0, 0)}, {"nr": 320}, 2, (0, 1, 3, 4, 7), [1.2], 22, 0, 1, "aaaaqqpp"
VSHARE = {(RO - 1, 1, 2): 1, (RO - 1, 1, 4): 1}
f32, b16, f16, i32, u16 = "float32", "bfloat16", "float16", "int32", "uint16"
SCRATCH = {}
for _n, _w, _d in (("IW", 164, f32), ("Zr", 128, f32), ("km", 512, b16), ("k1", 512, b16), ("c16", 128, f32), ("c32", 128, f32), ("cl", 64, f32), ("ri", 6, i32), ("cf", 32, f32),
                   ("Ib", 128, b16), ("nI", 128, f32), ("I2", 128, f32), ("nIb", 128, b16), ("B", 144, b16), ("Z0", 128, b16), ("Z1", 128, b16), ("zc", 64, b16),
                   ("AM", 512, f32), ("AH", 512, f16), ("GM", 512, f16), ("HM", 256, f32), ("SM", 256, f32), ("EMf", 128, f32), ("EM", 128, b16), ("DM", 8, b16),
                   ("O32e", 128, f32), ("kc", 2, b16), ("TC", 14, f32), ("CV", 38, b16), ("CK", 38, b16), ("msk", 512, b16), ("rv", 38, f32), ("rE", 38, f32),
                   ("KR", 64, f32), ("KH", 64, f32), ("SP", 132, f32), ("dl", 128, b16), ("ci", 132, i32), ("cfl", 132, f32), ("y1", 2048, f32), ("s", 8192, b16),
                   ("finA", 132, f32), ("fin", 132, f32), ("Pb", 8208, b16), ("E", 1024, b16), ("Mx", 512, b16), ("I", 512, f32), ("Ih", 512, f16), ("Wh", 512, f16)):
    SCRATCH[_n] = ("sbuf", [128, _w], _d)
for _f in (0, 1):
    for _n, _w, _d in (("P", 4096, f32), ("V", NV, b16), ("gi", 2048, i32), ("w", 8192, b16), ("W", 584 * RO + 584, f32), ("SB", 64 * RO, f16), ("Wa", 64 * RO + 64, f16), ("Xh", 64, f16), ("D", 164 * RO, f32),
                       ("Ou", 512, u16), ("U", 544, b16), ("unx", 512, b16), ("unb", 512, b16), ("pr", 512, b16), ("Lu", 4, u16),
                       ("g1", 32, b16), ("less", 32, b16), ("Lc", 32, u16), ("ev", 38, f32), ("J", 2, u16), ("q", 8, f32), ("Cu", 32, u16), ("LT", 64, f32),
                       ("Eb", 38, f32), ("nr", 38, f32), ("TT", 32, f32), ("Y", 132, f32), ("T8", 8, u16), ("up", 128, b16), ("X", 64, f32)):
        SCRATCH[_n + str(_f)] = ("sbuf", [128, _w], _d)
    for _b in range(4):
        SCRATCH["ps%d%d" % (_f, _b)] = ("psum", [128, 512], f32)
SEMAPHORES = ["eV", "eA", "eP", "eG", "sent", "ldc", "stv0", "stv1", "sto"] + ["ld%s%d" % (a, f) for a in "vgh" for f in (0, 1)] \
    + ["arr%s%d%d" % (a, t, f) for a in "ab" for t in range(1, RO) for f in (0, 1)]

CY, GA, SCAT, PEF = 0.9, 1.56, 3.8, 0.5
LAT, OWN, NET = 130.0, 220.0, 2300.0


def build(T, dst_addr, emask, nen):
    ops = []

    def op(eng, fn, rd, wr, cyc, bank=None, sem=None, inc=1, gn=0, sn=0, fx=0.0):
        c = NET if eng == "N" else (cyc * (PEF if eng == "P" else 1) + gn * GA + sn * SCAT) * CY + fx
        ops.append({"e": eng, "fn": fn, "rd": rd, "wr": wr, "c": c, "bk": bank, "sem": sem, "inc": inc, "cyc": cyc, "gn": gn, "sn": sn, "fx": fx})

    def V(fn, rd, wr, n=64, bank=None, gn=0, sn=0):
        if gn or sn:
            op("V", fn, rd, wr, 0, bank, gn=gn, sn=sn, fx=50.0)
        else:
            op("V", fn, rd, wr, max(n, 64), bank, fx=2.0)

    def ts(out, a, s1, s2, o0, o1, rd, wr, n=64, bank=None, gn=0):
        if o1 is None:
            V(lambda e: e.tensor_scalar(out, a, s1, None, o0), rd, wr, n, bank, gn)
        else:
            V(lambda e: e.tensor_scalar(out, a, s1, s2, o0, o1), rd, wr, n, bank, gn)

    def tt(out, a, b, o, rd, wr, n=64, bank=None, gn=0):
        V(lambda e: e.tensor_tensor(out, a, b, o), rd, wr, n, bank, gn)

    def cp(out, a, rd, wr, n=64, bank=None, gn=0, sn=0):
        V(lambda e: e.tensor_copy(out, a), rd, wr, n, bank, gn, sn)

    def ms(out, c, wr, n=64):
        V(lambda e: e.memset(out, c), [], wr, n)

    def scan(out, d0, d1, o0, o1, rd, wr, n=64, bank=None, init=0.0):
        V(lambda e: e.tensor_tensor_scan(out, d0, d1, init, o0, o1), rd, wr, n, bank)

    def tr(out, a, rd, wr, n=64, bank=None):
        V(lambda e: e.transpose(out, a), rd, wr, n, bank)

    def mm(out, l, r, st, sp, rd, bank, n=64, wide=False):
        op("P", lambda e: e.matmul(out, l, r, st, sp), rd, [], max(n, 64) * (4 if wide else 1), bank)

    def act(out, a, rd, wr, n, bias=0.0, scale=1.0, bank=None, func=F.Identity):
        op("A", lambda e: e.activation(out, a, func, bias=bias, scale=scale), rd, wr, n, bank, fx=65.0)

    def gat(out, a, rd, wr, n, bias=None):
        if bias is None:
            op("A", lambda e: e.activation(out, a, F.Copy), rd, wr, 0, gn=n, fx=65.0)
        else:
            op("A", lambda e: e.activation(out, a, F.Identity, bias=bias), rd, wr, 0, gn=n, fx=65.0)

    def io(out, pat, base, cm, wr, n, flag=True):
        if flag:
            op("G", lambda e: e.iota(out, pat, base, cm, allow_small_or_imprecise_dtypes=True), [], wr, 2 * n, fx=130.0)
        else:
            op("G", lambda e: e.iota(out, pat, base, cm), [], wr, 2 * n, fx=130.0)

    def move(out, a, n, rd, wr):
        op("G", lambda e: e.affine_select(out, a, [[0, n]], A.is_ge, 0.0, 0, 0), rd, wr, 2 * n, fx=170.0)

    def put(out, a, pat, base, val, rd, wr, n=128):
        op("G", lambda e: e.affine_select(out, a, pat, A.not_equal, val, base, 1), rd, wr, 2 * n, fx=170.0)

    def dma(q, out, a, rd, wr, sem, lat):
        op(q, lambda e: e.dma_start(out, a), rd, wr, 0, "dma" + q, sem, 16, fx=100.0)
        ops[-1]["lat"] = lat

    def later(first, how=1):
        for o in ops[first:]:
            o["bulk"] = how

    dma("S", T.ci[:, 0:64], T.par[:], [], ["ci0"], "ldc", 2200)
    dma("S", T.ci[:, 64:128], T.cla[:], [], ["ci1"], "ldc", 2200)
    dma("S", T.ci[:, 128:132], T.lit[:], [], ["ci2"], "ldc", 2200)
    for f in (0, 1):
        for nm, src, buf, c0, a, b, at in (("g", T.gen, T["gi%d" % f], 0, 0, 1024, 2200), ("h", T.gen, T["gi%d" % f], 0, 1024, 2048, 3000),
                                           ("v", T.val, T["V%d" % f], PAD, 0, 4096, 4200)):
            for j in range(8):
                gr = 2 * (j // 2) + f
                dma("A" if f == 0 and j % 2 else "S", buf[16 * j:16 * j + 16, c0 + a:c0 + b], src[16 * gr:16 * gr + 16, a:b],
                    ["ldv0%d" % z for z in range(8)] if f else [], ["ld%s%d%d" % (nm, f, j)],
                    "ld%s%d" % (nm, f), at + (300 if nm == "v" else 150) * j)
    io(T.ri[:, 0:1], [[0, 1]], 0, 1, ["ri"], 1, False)
    io(T.c16[:], [[16, 8], [0, 16]], 0, 0, ["c16"], 128)
    ms(T.Zr[:], 0.0, ["Zr"], 128)
    I32 = T.IW[:, 0:128]
    AM = lambda x, y: T.AM[:, 256 * x + 128 * y:256 * x + 128 * y + 128]
    AH = lambda x, y: T.AH[:, 256 * x + 128 * y:256 * x + 128 * y + 128]
    GM = lambda x: T.GM[:, 128 * x:128 * x + 128]
    HM = lambda x: T.HM[:, 128 * x:128 * x + 128]
    SM = lambda x: T.SM[:, 128 * x:128 * x + 128]
    hop = lambda x, y: ([[-32, 4], [1000, 2], [-1, 16]], -16 * x - 1000 * y)
    for x in (0, 1):
        for y in (0, 1):
            put(AM(x, y), T.Zr[:], *hop(x, y), 1.0, ["Zr"], ["A%d%d" % (x, y)])
    put(T.Ib[:], T.Zr[:], [[-1, 128]], 0, 1.0, ["Zr"], ["Ib"])
    for j, m in enumerate((15, 16, 112, 96)):
        ts(T.ri[:, j + 1:j + 2], T.ri[:, 0:1], m, None, A.bitwise_and, None, ["ri"], ["ri%d" % j])
    cf = T.cf
    col = lambda j: cf[:, j:j + 1]
    cp(cf[:, 0:5], T.ri[:, 0:5], ["ri"] + ["ri%d" % j for j in range(4)], ["cf"])
    cp_, ch, c16r, c32r = [col(j) for j in range(1, 5)]
    cp(T.AH[:], T.AM[:], ["A00", "A01", "A10", "A11"], ["AH"], 512)
    ts(T.Z0[:], T.c16[:], c16r, 16384.0, A.is_equal, A.mult, ["c16", "cf"], ["Z0"], 128)
    ts(T.Z1[:], T.c16[:], c16r, -16384.0, A.is_equal, A.mult, ["c16", "cf"], ["Z1"], 128)
    ms(T.zc[:], -8.5 * 16384, ["zc"]); ms(T.zc[:, 32:64], 8.5 * 16384, ["zc"])
    ts(T.cfl[:, 0:128], T.ci[:, 0:128], -CB, None, A.add, None, ["ci0", "ci1", "ci2"], ["cfl"], 128)
    ts(T.cfl[:, 128:132], T.ci[:, 128:132], OFF, None, A.add, None, ["ci0", "ci1", "ci2"], ["cfm"])
    ms(T.msk[:], 1.0, ["msk"], 256); ms(T.msk[:, 0:512:16], 0.0, ["msk"])
    ms(T.Pb[:, 0:1], 0.0, ["Pb0"])
    first = len(ops)
    io(T.c32[:], [[32, 4], [0, 32]], 0, 0, ["c32"], 128)
    io(T.cl[:], [[16, 2], [32, 2], [1, 16]], 0, 0, ["cl"], 64)
    io(T.CK[:], [[0, 2], [-1, 19]], 15, 0, ["CK"], 38)
    put(I32, T.Zr[:], [[-1, 128]], 0, 1.0, ["Zr"], ["IW"])
    put(T.nI[:], T.Zr[:], [[-1, 128]], 0, -1.0, ["Zr"], ["nI"])
    put(T.nIb[:], T.Zr[:], [[-1, 128]], 0, -1.0, ["Zr"], ["nIb"])
    if "q" in PB or "p" in PB:
        put(T.I2[:], T.Zr[:], [[-1, 128]], 0, 2.0, ["Zr"], ["I2"])
    for x in (0, 1):
        put(HM(x), T.Zr[:], [[-32, 4], [0, 2], [-1, 16]], -16 * x, 1.0, ["Zr"], ["H%d" % x])
        put(SM(x), T.Zr[:], [[-32, 4], [0, 32]], -2 - x, 1.0, ["Zr"], ["S%d" % x])
        put(SM(x), SM(x), [[-32, 4], [0, 32]], -4 - x, -BIG, ["S%d" % x], ["S%d" % x])
        put(GM(x), AM(x, 0), hop(x, 0)[0], -16 * x - 1, -1.0, ["A%d0" % x], ["G%d" % x])
        put(T.GM[:, 128 * x + 15:128 * x + 128:32], T.Zr[:, 0:4], [[-32, 4]], -16 * x - 15, 1.0, ["Zr", "G%d" % x], ["G%d" % x], 4)
        put(T.GM[:, 128 * x + 19:128 * x + 128:32], T.Zr[:, 0:4], [[-32, 4]], -16 * x, 1.0, ["Zr", "G%d" % x], ["Gx%d" % x], 4)
    ts(col(8), ch, 2.0, cp_, A.mult, A.add, ["cf"], ["own0"])
    ts(col(9), col(8), 16.0, None, A.add, None, ["own0"], ["own1"])
    for x in (0, 1):
        ts(T.EMf[:, 64 * x:64 * x + 64], T.cl[:], col(8 + x), -BIG, A.subtract, A.mult, ["cl", "own0", "own1"], ["EM%d" % x])
    ts(T.EM[:], T.EMf[:], BIG, None, A.min, None, ["EM0", "EM1"], ["EM"], 128)
    ms(T.B[:], 0.0, ["B"])
    ts(T.B[:, 16:144:16], T.c16[:, 0:128:16], c16r, 2048.0, A.is_equal, A.mult, ["c16", "cf"], ["B"])
    io(T.DM[:], [[64, 2], [0, 4]], 0, 0, ["DM"], 8)
    ms(T.CV[:], 0.0, ["CV"])
    ts(col(17), cp_, -32.0, -16.0, A.mult, A.add, ["cf"], ["cv0"])
    for q in (0, 1):
        ts(T.CV[:, 19 * q + 1:19 * q + 17], T.c16[:, 16 * q:16 * q + 16], -1.0, col(17), A.mult, A.add, ["c16", "cv0", "CV"], ["CV%d" % q])
    for t in range(RO):
        io(T.TC[:, 2 * t:2 * t + 2], [[-16, 2]], 2048 * AT[t] - 529, 0, ["TB%d" % t], 2)
    ts(T.TC[:, 0:2 * RO], T.TC[:, 0:2 * RO], cp_, None, A.subtract, None, ["cf"] + ["TB%d" % t for t in range(RO)], ["TC"])
    ts(T.O32e[:], T.c32[:], c32r, 2048.0, A.is_equal, A.mult, ["c32", "cf"], ["O32e"], 128)
    ms(T.kc[:], -1024.0, ["kc"])
    ms(T.rv[:], 1.0, ["rv"]); ms(T.rv[:, 0:38:19], -1.0e11, ["rv"]); ms(T.rv[:, 18:38:19], M2K, ["rv"])
    ms(T.rE[:], 1.0e9, ["rE"]); ms(T.rE[:, 0:38:19], 512.0, ["rE"])
    io(T.dl[:], [[-64, 2], [0, 64]], 32, 0, ["dl"], 128)
    ms(T.KR[:], 0.0, ["KR"])
    for j, c in ((15, CB + OFF), (16, -32.0), (17, M2), (18, -M2), (19, CB + OFF)):
        ms(T.KR[:, j:64:32], c, ["KR%d" % j])
        ops[-1]["rd"] = ["KR"]
    tr(T.KH[:], T.KR[:], ["KR%d" % j for j in range(15, 20)], ["KH"])
    io(T.SP[:, 0:128], [[0, 128]], 0, 0, ["SP"], 128)
    ms(T.SP[:, 130:132], 0.0, ["SP2"])
    ts(T.SP[:, 128:130], cf[:, 8:10], 0.5, None, A.add, None, ["own0", "own1"], ["SP1"])
    ms(T.km[:], -M4, ["km"], 256)
    ms(T.k1[:], 1.0, ["k1"], 256)
    later(first, CONB)
    POFF = [0.0 if PB[4 * f] in "gG" else OFF for f in (0, 1)]
    AK = ["A00", "A01", "A10", "A11"]

    def phase_setup(f):
        B = lambda n: T[n + str(f)]
        k = lambda n: n + str(f)
        ps = [T["ps%d%d" % (f, b)] for b in range(4)]
        bk = ["bk%d%d" % (f, b) for b in range(4)]
        W = B("W")
        ms(B("V")[:, 0:PAD], 0.0, [k("V")], PAD // 2)
        for j in (0, 1):
            for h in (0, 1):
                for q in (0, 1):
                    mm(ps[2][:, 32 * j + 16 * h:32 * j + 16 * h + 16], AM(f, q), T.cfl[:, 64 * j + 2 * h + q:64 * j + 64:4], q == 0, q == 1,
                       ["cfl"] + AK, bk[2], 16, True)
        for h in (0, 1):
            mm(ps[2][:, 64:66], AM(f, h), T.cfl[:, 128 + 2 * h:130 + 2 * h], h == 0, h == 1, ["cfm"] + AK, bk[2], 2, True)
        tr(W[:, 512:576], ps[2][:, 0:64], [], [k("in0")], 64, bk[2])
        cp(W[:, 576:578], ps[2][:, 64:66], [], [k("in0a")], 64, bk[2])
        q_ = B("q")
        ts(q_[:, 4:6], W[:, 576:578], M2, -M2 - 32, A.add, A.add, [k("in0a")], [k("r0")])
        for q in (0, 1):
            ts(W[:, 578 + q:579 + q], q_[:, 4 + q:5 + q], 2.0, W[:, 576 + q:577 + q], A.mult, A.subtract, [k("r0"), k("in0a")], [k("in0b%d" % q)])
        first = len(ops)
        ms(B("U")[:, 512:544], 0.0, [k("Up")])
        io(B("unx")[:], [[0, 512]], 0, 0, [k("unx")], 512)
        io(B("D")[:], [[0, 164 * RO]], 0, 0, ["Dz%d%d" % (t, f) for t in range(RO)], 164 * RO)
        later(first, CONB)
        P = B("P")
        first = len(ops)
        for i in range(4):
            ev, od = P[:, 1024 * i:1024 * i + 1024:2], P[:, 1024 * i + 1:1024 * i + 1024:2]
            y = T.y1[:, 512 * i:512 * i + 512]
            b = 3 * (i % 2)
            how = PB[4 * f + i]
            ld = ["ld%s%d%d" % ("gh"[i // 2], f, j) for j in range(8)]
            if how in "gG":
                move(ev, B("gi")[:, 512 * i:512 * i + 512], 512, ld, [k("Pe%d" % i)])
                act(y, ev, [k("Pe%d" % i)], ["y%d" % i], 512, M4, 1.9998)
                mm(ps[b][:], I32, y, True, False, ["IW", "y%d" % i], bk[b], 512, True)
                mm(ps[b][:], T.Ib[:], T.km[:], False, False, ["Ib", "km"], bk[b], 512)
                mm(ps[b][:], T.Ib[:], T.k1[:], False, False, ["Ib", "k1"], bk[b], 512)
                mm(ps[b][:], T.nI[:], ev, False, True, ["nI", k("Pe%d" % i)], bk[b], 512, True)
                if how == "G":
                    act(od, ps[b][:], [], [k("Po%d" % i)], 512, 0.0, 1.0, bk[b])
                else:
                    cp(od, ps[b][:], [], [k("Po%d" % i)], 512, bk[b])
                continue
            ts(ev, B("gi")[:, 512 * i:512 * i + 512], POFF[f], None, A.add, None, ld, [k("Pe%d" % i)], 512)
            if how == "a":
                act(y, ev, [k("Pe%d" % i)], ["y%d" % i], 512, M4, 2.0)
                act(ps[b][:], y, ["y%d" % i], [], 512, -M4, 1.0, bk[b])
                tt(od, ps[b][:], ev, A.subtract, [k("Pe%d" % i)], [k("Po%d" % i)], 512, bk[b])
            else:
                ts(y, ev, M2, -M2, A.add, A.add, [k("Pe%d" % i)], ["y%d" % i], 512)
                mm(ps[b][:], T.I2[:], y, True, False, ["I2", "y%d" % i], bk[b], 512, True)
                mm(ps[b][:], T.nI[:], ev, False, True, ["nI", k("Pe%d" % i)], bk[b], 512, True)
                if how == "p":
                    act(od, ps[b][:], [], [k("Po%d" % i)], 512, 0.0, 1.0, bk[b])
                else:
                    cp(od, ps[b][:], [], [k("Po%d" % i)], 512, bk[b])
        later(first, f * P1B)

    def phase(t, f):
        B = lambda n: T[n + str(f)]
        k = lambda n: n + str(f)
        ps = [T["ps%d%d" % (f, b)] for b in range(4)]
        bk = ["bk%d%d" % (f, b) for b in range(4)]
        w0, s0, d0 = 584 * t, 64 * t, 164 * t
        W, SB, D, q_, LT, Y = B("W"), B("SB"), B("D"), B("q"), B("LT"), B("Y")
        Wc = lambda a, b: W[:, w0 + a:w0 + b]
        Sc = lambda a, b: SB[:, s0 + a:s0 + b]
        Dc = lambda a, b, c=1: D[:, d0 + a:d0 + b:c] if c > 1 else D[:, d0 + a:d0 + b]
        INL = [k("in0a"), k("in0b0"), k("in0b1")] if t == 0 else [k("inb%d_" % t)]
        INC = [k("in0") if t == 0 else k("ina%d_" % t)]
        came = Wc(512, 576) if t == 0 else B("Wa")[:, s0:s0 + 64]
        VK = [k("V")] + (["ldv%d%d" % (f, j) for j in range(8)] if t == 0 else [])
        PK = [k("P%s%d" % (a, i)) for a in "eo" for i in range(4)]
        Vw = B("V")[:, 0:NV]
        sb = lambda n: "%s%d%d" % (n, t, f)

        def send(part, dst, src, rd):
            if t + 1 < RO:
                sem = "arr%s%d%d" % (part, t + 1, f)
                op("G", lambda e: e.remote_dma(dst, src, T.sem[sem], T.sem.sent, dst_addr[1], dst_addr[0], emask),
                   rd, [sb("gone" + part)], 0, None, "sent", 0, fx=300.0)
                op("N", None, [sb("gone" + part)], [k("in%s%d_" % (part, t + 1))], 0, None, sem, nen)

        ts(B("Lu")[:], Wc(576, 580), 0.5, None, A.add, None, INL, [k("Lu")])
        cp(B("g1")[:], B("V")[:, 64:NV].indirect(B("Lu")[:, 2:4]), VK + [k("Lu")], [k("g1")], gn=32)
        tt(B("less")[:], Vw.indirect(B("Lu")[:, 0:2]), B("g1")[:], A.is_lt, VK + [k("Lu"), k("g1")], [k("less")], gn=32)
        for x in (0, 1):
            o = ps[2][:, 300 + 32 * x:332 + 32 * x]
            mm(o, T.Ib[:], T.zc[:, 32 * x:32 * x + 32], True, False, ["Ib", "zc"], bk[2])
            mm(o, T["Z%d" % x][:], B("less")[:], False, True, ["Z0", "Z1", k("less")], bk[2])
        tt(B("X")[:], ps[2][:, 300:364], came, A.min, INC, [k("XX")], 64, bk[2])
        tt(Sc(0, 32), B("X")[:, 0:32], B("X")[:, 32:64], A.max, [k("XX")], [sb("c")])
        for x in (0, 1):
            for y in (0, 1):
                mm(ps[2][:, 32 + x:64:2], AH(x, y), Sc(16 * y, 16 * y + 16), y == 0, y == 1, [sb("c"), "AH"], bk[2], 16)
        ts(B("Lc")[:], ps[2][:, 32:64], CB, None, A.add, None, [], [k("Lc")], 64, bk[2])
        if t:
            move(Wc(512, 544), B("Wa")[:, s0:s0 + 32], 32, INC + [k("Lc")], [sb("Dw")])
            ops[-1]["bulk"] = 1
        for u, (a, b) in enumerate(zip([0] + IMG, IMG + [32])):
            src = B("P")[:, 0:4096].indirect(B("Lc")[:, a:b])
            ou = [k("Ou_%d_" % z) for z in range(a, b)]
            n = 16 * (b - a)
            if (t, f) in IMG_ACT:
                gat(T.I[:, 16 * a:16 * b], src, PK + [k("Lc")], ["I%d" % u], n, -POFF[f] - CB)
                tr(Wc(16 * a, 16 * b), T.I[:, 16 * a:16 * b], ["I%d" % u], [sb("O%d" % u)], n)
                ts(B("Ou")[:, 16 * a:16 * b], Wc(16 * a, 16 * b), CB + PAD, None, A.add, None, [sb("O%d" % u)], ou, n)
            else:
                ts(T.Ih[:, 16 * a:16 * b], src, -POFF[f] - CB, None, A.add, None, PK + [k("Lc")], ["Ih%d" % u], gn=n)
                tr(T.Wh[:, 16 * a:16 * b], T.Ih[:, 16 * a:16 * b], ["Ih%d" % u], ["Wh%d" % u], n // 2)
                ts(B("Ou")[:, 16 * a:16 * b], T.Wh[:, 16 * a:16 * b], CB + PAD, None, A.add, None, ["Wh%d" % u], ou, n // 2)
                if u:
                    later(len(ops) - 3, IMGB[u - 1])
                move(Wc(16 * a, 16 * b), T.Wh[:, 16 * a:16 * b], n, ["Wh%d" % u], [sb("O%d" % u)])
                ops[-1]["bulk"] = 1
        a0 = held = 0
        UK = []
        for ci, n in enumerate(CHUNKS):
            nv = VSHARE.get((t, f, ci), 0)
            lk = lambda nm, a, b: [k("%s_%d_" % (nm, x)) for x in range(a, b)]
            ou = lk("Ou", a0, a0 + n)
            if nv < n:
                gat(B("w")[:, 256 * a0:256 * (a0 + n - nv)], Vw.indirect(B("Ou")[:, 16 * a0:16 * (a0 + n - nv)]), VK + ou, lk("w", a0, a0 + n - nv), 256 * (n - nv))
                ops[-1]["bulk"] = 1
                ops[-1]["bk"] = "gathers"
            if nv:
                cp(B("w")[:, 256 * (a0 + n - nv):256 * (a0 + n)], Vw.indirect(B("Ou")[:, 16 * (a0 + n - nv):16 * (a0 + n)]), VK + ou, lk("w", a0 + n - nv, a0 + n), gn=256 * nv)
                ops[-1]["bulk"] = 1
            mx = T.Mx[:, 16 * a0:16 * (a0 + n)]
            mk_ = ["Mx_%d" % z for z in range(a0, a0 + n)]
            short = ci >= len(CHUNKS) - SHORT
            for a in range(a0, a0 + n, PIECE):
                b = min(a + PIECE, a0 + n)
                ne = 128 * (b - a)
                if short:
                    e0 = 256 * (a - 32 + sum(CHUNKS[-SHORT:]))
                    e1 = e0 + 256 * (b - a)
                    ek = ["E_%d" % z for z in range(a, b)]
                    scan(T.E[:, e0:e1], B("w")[:, 256 * a - 1:256 * b - 1], T.msk[:, 0:256 * (b - a)], A.max, A.mult, lk("w", a - 1, b) + ["msk"], ek, ne)
                    ops[-1]["bulk"] = 1
                    scan(T.s[:, 256 * a:256 * b], B("w")[:, 256 * a:256 * b], T.E[:, e0:e1], A.max, A.min, lk("w", a, b) + ek, ["s_%d" % z for z in range(a, b)], ne)
                    ops[-1]["bulk"] = 1
                    if b == a0 + n:
                        tt(mx, T.E[:, e1 - 256 * n + 15:e1:16], B("w")[:, 256 * a0 + 15:256 * b:16], A.max, lk("w", a0, b) + ["E_%d" % z for z in range(a0, b)], mk_, 32 * n)
                else:
                    scan(T.Pb[:, 256 * a + 1:256 * b + 1], T.msk[:, 0:256 * (b - a)], B("w")[:, 256 * a:256 * b], A.mult, A.max, lk("w", a, b) + ["msk"],
                         ["Pb_%d" % z for z in range(a, b)], ne)
                    ops[-1]["bulk"] = 1
            if not short:
                tops = T.Pb[:, 256 * a0 + 16:256 * (a0 + n) + 1:16]
                pk = ["Pb_%d" % z for z in range(a0, a0 + n)]
                move(mx, tops, 16 * n, pk, mk_)
                io(tops, [[0, 16 * n]], 0, 0, pk, 16 * n)
                for a in range(a0, a0 + n, PIECE):
                    b = min(a + PIECE, a0 + n)
                    scan(T.s[:, 256 * a:256 * b], B("w")[:, 256 * a:256 * b], T.Pb[:, 256 * a:256 * b], A.max, A.min,
                         lk("w", a, b) + ["Pb_%d" % z for z in range(max(a - 1, 0), b)] + ["Pb0"], ["s_%d" % z for z in range(a, b)], 128 * (b - a))
                    ops[-1]["bulk"] = 1
            if ci in JOIN:
                held, a0 = held + n, a0 + n
                continue
            a0, n, held = a0 - held, n + held, 0
            db = 3 * (len([z for z in range(ci + 1, len(CHUNKS)) if z not in JOIN]) % 2)
            dps = ps[db][:, 16 * a0:16 * (a0 + n)]
            mm(dps, T.Ib[:], T.Mx[:, 16 * a0:16 * (a0 + n)], True, False, ["Mx_%d" % z for z in range(a0, a0 + n)] + ["Ib"], bk[db], 16 * n)
            mm(dps, T.nIb[:], T.s[:, 256 * a0 + 15:256 * (a0 + n):16], False, True, ["s_%d" % z for z in range(a0, a0 + n)] + ["nIb"], bk[db], 16 * n)
            uk = k("U%d" % ci)
            UK.append(uk)
            if ci < UNIT_ACT.get((t, f), UNIT_DEF):
                act(B("U")[:, 16 * a0:16 * (a0 + n)], dps, [], [uk], 16 * n, -256.0 * (MT[t] + 0.5), 256.0, bk[db], F.Sigmoid)
            else:
                ts(B("U")[:, 16 * a0:16 * (a0 + n)], dps, MT[t] + 0.5, None, A.is_gt, None, [], [uk], 16 * n, bk[db])
            for p in range(a0 // 2, (a0 + n) // 2):
                if p == 0:
                    mm(ps[1][:, 0:38], T.Ib[:], T.CV[:], True, False, ["Ib", "CV0", "CV1"], bk[1])
                    mm(ps[1][:, 0:38:19], I32, T.TC[:, 2 * t:2 * t + 2], False, False, ["IW", "TC"], bk[1], 2, True)
                    for q in range(2 if t else 0):
                        for x in (0, 1):
                            mm(ps[1][:, 19 * q:19 * q + 1], T.O32e[:], Dc(x - 28, x - 27), False, False, ["O32e", "pro%d%d" % (t - 1, f)], bk[1], 1, True)
                        mm(ps[1][:, 19 * q:19 * q + 1], T.nI[:], q_[:, 2:3], False, False, ["nI", k("a1")], bk[1], 1, True)
                for q in (0, 1):
                    mm(ps[1][:, 19 * q + 1:19 * q + 17], T.B[:, 16 - p:144 - p], B("U")[:, 32 * p + 16 * q:32 * p + 16 * q + 16], False, p == 15 and q == 1, ["B", uk], bk[1])
            a0 += n
        ev = B("ev")
        scan(ev[:], T.rv[:], ps[1][:, 0:38], A.add, A.max, ["rv"], [k("ev")], 64, bk[1])
        for q in (0, 1):
            ts(B("J")[:, q:q + 1], ev[:, 19 * q + 18:19 * q + 19], -M2K, ev[:, 19 * q + 17:19 * q + 18], A.add, A.subtract, [k("ev")], [k("J%d" % q)])
        JK = [k("J0"), k("J1")]
        OK = [sb("O%d" % u) for u in range(len(IMG) + 1)] + JK + ([sb("Dw")] if t else INC)
        cp(B("unx")[:, 0:512:16], B("U")[:, 0:544].indirect(B("J")[:, 0:2]), UK + [k("Up")] + JK, [k("unx")], gn=32)
        cp(Sc(32, 64), Wc(0, 544).indirect(B("J")[:, 0:2]), OK, [sb("C")], gn=32)
        ts(Dc(136, 138), B("J")[:], 511.5, None, A.is_lt, None, JK + [sb("Dz")], [sb("pro")])
        send("a", B("Wa")[:, s0 + 64:s0 + 128], Sc(0, 64), [sb("c"), sb("C")])
        ts(B("Cu")[:], Sc(32, 64), CB + PAD, None, A.add, None, [sb("C")], [k("Cu")])
        scan(B("unb")[:], T.msk[:, 0:512], B("unx")[:], A.mult, A.add, ["msk", k("unx")], [k("unb0"), k("unb1")], 256)
        mm(ps[2][:, 64:128], I32, T.KH[:], True, False, ["IW", "KH"], bk[2], 64, True)
        for q in (0, 1):
            for h in (0, 1):
                mm(ps[2][:, 64 + 32 * q + 16 * h:80 + 32 * q + 16 * h], GM(h), Sc(32 + 16 * q, 48 + 16 * q), False, h + q == 2, [sb("C"), "Gx0", "Gx1"], bk[2], 16)
        tr(LT[:], ps[2][:, 64:128], [], [k("LT")], 64, bk[2])
        mm(ps[2][:, 264:266], I32, Wc(576, 578), True, False, ["IW"] + INL, bk[2], 2, True)
        mm(ps[2][:, 264:266], T.nI[:], LT[:, 19:64:32], False, True, ["nI", k("LT")], bk[2], 2, True)
        cd = ps[1][:, 64:102]
        mm(cd, T.Ib[:], T.CK[:], True, False, ["Ib", "CK"], bk[1])
        for q in (0, 1):
            tt(B("pr")[:, 256 * q:256 * q + 256], Vw.indirect(B("Cu")[:, 16 * q:16 * q + 16]), B("unb")[:, 256 * q:256 * q + 256], A.mult,
               VK + [k("Cu"), k("unb%d" % q)], [k("pr%d" % q)], gn=256)
            for p in range(16):
                mm(ps[1][:, 64 + 19 * q:80 + 19 * q], T.B[:, 16 - p:144 - p], B("pr")[:, 256 * q + 16 * p:256 * q + 16 * p + 16], False, p + q == 16, ["B", k("pr%d" % q)], bk[1])
        scan(B("Eb")[:], T.rE[:], cd, A.min, A.max, ["rE"], [k("Eb")], 64, bk[1], 1.0e9)
        tt(B("nr")[:], cd, B("Eb")[:], A.is_lt, [k("Eb")], [k("nr")], 64, bk[1])
        for q in (0, 1):
            scan(Dc(98 + q, 136, 2), B("nr")[:, 19 * q:19 * q + 19], LT[:, 32 * q:32 * q + 19], A.mult, A.add, [k("nr"), k("LT"), sb("Dz")], [sb("l%d" % q)], 64, bk[2], ps[2][:, 264 + q:265 + q])
        LK = [sb("l0"), sb("l1")]
        for q in (0, 1):
            ts(Dc(130 + q, 131 + q), Dc(134 + q, 135 + q), 2.0, Dc(128 + q, 129 + q), A.mult, A.subtract, [sb("l%d" % q)], [sb("lp%d" % q)])
        PKK = [sb("lp0"), sb("lp1")]
        send("b", W[:, w0 + 584 + 576:w0 + 584 + 580], Dc(128, 132), PKK + LK)
        tr(B("TT")[:], Dc(132, 164), LK + [sb("pro"), sb("Dz")], [k("TT")])
        mm(ps[3][:, 0:128], T.Ib[:], T.EM[:], True, False, ["Ib", "EM"], bk[3], 128)
        for q in (0, 1):
            for x in (0, 1):
                mm(ps[3][:, 64 * q + 32 * x:64 * q + 32 * x + 32], SM(x), B("TT")[:], False, q + x == 2, ["S0", "S1", k("TT")], bk[3], 32, True)
        mm(ps[0][:, 0:8], T.Ib[:], T.DM[:], True, False, ["Ib", "DM"], bk[0])
        for q in (0, 1):
            ts(Dc(q, 128, 2), ps[3][:, 64 * q:64 * q + 64], Dc(134 + q, 135 + q), 32768.0, A.not_equal, A.mult, LK, [sb("ne%d" % q)], 64, bk[3])
        for q in (0, 1):
            scan(Y[:, q:132:2], T.SP[:, q:132:2], Dc(q, 132, 2), A.max, A.min, ["SP", "SP1", "SP2", sb("ne%d" % q), sb("lp%d" % q)], [k("Y%d" % q)], 66, None, 32768.0)
        for x in (0, 1):
            mm(ps[0][:, x:8:2], HM(x), Y[:, 128:132], False, x == 1, ["H0", "H1", k("Y0"), k("Y1")], bk[0], 4, True)
        ts(B("T8")[:], ps[0][:, 0:8], 0.5, None, A.add, None, [], [k("T8")], 64, bk[0])
        ts(B("up")[:, 0:64], Vw.indirect(B("T8")[:, 0:4]), 223.0, None, A.min, None, VK + [k("T8")], [k("up")], gn=64)
        ts(B("up")[:, 64:128], Vw.indirect(B("T8")[:, 4:8]), 32.0, None, A.max, None, VK + [k("T8")], [k("dn")], gn=64)
        V(lambda e: e.tensor_tensor(Vw.indirect(B("T8")[:, 0:8]), B("up")[:], T.dl[:], A.add), VK[1:] + [k("up"), k("dn"), k("T8"), "dl"], [k("V")], sn=128)
        if t + 1 < RO:
            mm(ps[2][:, 128:129], T.Ib[:], T.kc[:, 0:1], True, False, ["Ib", "kc"], bk[2])
            for q in (0, 1):
                mm(ps[2][:, 128:129], T.O32e[:], Dc(136 + q, 137 + q), False, q == 1, ["O32e", sb("pro")], bk[2], 1, True)
            ts(q_[:, 2:3], ps[2][:, 128:129], M4K, -M4K, A.add, A.add, [], [k("a1")], 64, bk[2])
        else:
            tr(B("Xh")[:], Sc(0, 64), [sb("c"), sb("C")], [k("Xh")])
            for j in (0, 1):
                for h in (0, 1):
                    for q in (0, 1):
                        mm(ps[2][:, 128 + 64 * j + 2 * h + q:192 + 64 * j:4], AH(q, f), B("Xh")[:, 32 * j + 16 * h:32 * j + 16 * h + 16], True, True,
                           [k("Xh"), "AH"], bk[2], 16)
            if f == 0:
                ts(T.finA[:, 0:128], ps[2][:, 128:256], CB, None, A.add, None, [], ["finA"], 128, bk[2])
            else:
                tt(T.fin[:, 0:128], ps[2][:, 128:256], T.finA[:, 0:128], A.add, ["finA"], ["fin"], 128, bk[2])
                dma("S", T.yd[:], T.fin[:, 0:64], ["fin"], [], "sto", 2000)
                dma("S", T.yc[:], T.fin[:, 64:128], ["fin"], [], "sto", 2000)
            for h in (0, 1):
                mm(ps[2][:, 256 + 2 * h:258 + 2 * h], AM(h, f), Dc(128, 130), True, True, LK + AK, bk[2], 2, True)
            if f == 0:
                ts(T.finA[:, 128:132], ps[2][:, 256:260], -OFF, None, A.add, None, [], ["finB"], 64, bk[2])
            else:
                tt(T.fin[:, 128:132], ps[2][:, 256:260], T.finA[:, 128:132], A.add, ["finB"], ["finl"], 64, bk[2])
                dma("S", T.yl[:], T.fin[:, 128:132], ["finl"], [], "sto", 2000)
            for j in range(4):
                r0 = 32 * j + 16 * f
                dma("A" if f == 1 and j % 2 else "S", T.yv[r0:r0 + 16, :], B("V")[r0:r0 + 16, PAD:], [k("V")], [], "stv%d" % f, 3000)

    phase_setup(0)
    phase_setup(1)
    for t in range(RO):
        first = len(ops)
        phase(t, 0)
        if t + 1 == RO:
            late = [o for o in ops[first:] if o["e"] == "V" and not o.get("bulk")]
            for o in late[DEFER:]:
                o["bulk"] = 1.5
        phase(t, 1)
    return ops


def link(ops):
    lw, rdrs = {}, {}
    for i, o in enumerate(ops):
        hard, soft = set(), set()
        for key in o["rd"]:
            hard.add(lw[key])
        for key in o["wr"]:
            if key in lw:
                hard.add(lw[key])
            hard.update(rdrs.get(key, []))
        b = o["bk"]
        if b is not None:
            if b in lw:
                (soft if ops[lw[b]]["e"] == o["e"] else hard).add(lw[b])
            lw[b] = i
        for key in o["rd"]:
            rdrs.setdefault(key, []).append(i)
        for key in o["wr"]:
            lw[key] = i
            rdrs[key] = []
        hard.discard(i)
        o["hard"], o["soft"] = hard, soft - hard


def kind(o):
    return o["wr"][0].rstrip("0123456789_") if o["wr"] else ""


def schedule(ops):
    n = len(ops)
    succ = [[] for _ in ops]
    for i, o in enumerate(ops):
        for j in o["hard"] | o["soft"]:
            succ[j].append(i)
    pri = [0.0] * n
    for i in range(n - 1, -1, -1):
        o = ops[i]
        pri[i] = o["c"] + o.get("lat", 0) + max([pri[j] + ((OWN if ops[j]["e"] == o["e"] else LAT) if i in ops[j]["hard"] else 0) for j in succ[i]] + [0])
    left = [len(o["hard"] | o["soft"]) for o in ops]
    rdy = [0.0] * n
    free = {e: 0.0 for e in "VAPGSN"}
    cand = {e: [] for e in "VAPGSN"}
    for i in range(n):
        if left[i] == 0:
            cand[ops[i]["e"]].append(i)
    order = {e: [] for e in "VAPGSN"}
    end = 0.0
    busy = {e: 0.0 for e in "VAPGSN"}
    for _ in range(n):
        best = None
        for e in cand:
            if cand[e]:
                t0 = max(free[e], min(rdy[i] for i in cand[e]))
                if best is None or t0 < best[0]:
                    best = (t0, e)
        t0, e = best
        i = max((i for i in cand[e] if rdy[i] <= t0), key=lambda i: pri[i] - BULK * ops[i].get("bulk", 0))
        if ops[i].get("bulk"):
            soon = [j for j in cand[e] if rdy[j] <= t0 + WAIT.get(kind(ops[j]), LOOK) and not ops[j].get("bulk")]
            if soon:
                i = min(soon, key=lambda j: rdy[j])
        t0 = max(t0, rdy[i])
        cand[e].remove(i)
        o = ops[i]
        o["t0"] = t0
        done = t0 + o["c"]
        busy[e] += o["c"]
        if e != "N":
            free[e] = done
        order[e].append(i)
        fin = done + o.get("lat", 0)
        end = max(end, fin)
        for j in succ[i]:
            rdy[j] = max(rdy[j], fin + (OWN if ops[j]["e"] == e else LAT) if i in ops[j]["hard"] else done)
            left[j] -= 1
            if left[j] == 0:
                cand[ops[j]["e"]].append(j)
    return order, end, busy


def rank_program(g, core, T, topo):
    rank = T.rank_of(core)
    if rank is None:
        return
    nxt = T.cores[(rank + 1) % len(T.cores)]
    eng = topo.engines(core, nxt)
    ops = build(T, topo.addr(nxt), topo.mask(core, nxt), len(eng))
    link(ops)
    order, _, _ = schedule(ops)
    queue = {"V": g.vector, "A": g.scalar, "P": g.tensor, "G": g, "S": g.sync}
    total = {}
    for o in ops:
        if o["sem"]:
            total[o["sem"]] = total.get(o["sem"], 0) + o["inc"]
    total["sent"] = len(eng) * sum(1 for o in ops if o["sem"] == "sent")
    for e in "VAPG":
        c = 0
        for i in order[e]:
            if not ops[i]["sem"]:
                c += 1
                ops[i]["tick"] = ("e" + e, c)
        total["e" + e] = c
    for o in ops:
        if o["sem"]:
            o["tick"] = (o["sem"], total[o["sem"]])
    know = {e: {} for e in "VAPGS"}
    waits = {}
    for i in sorted(range(len(ops)), key=lambda i: (ops[i]["t0"], i)):
        o = ops[i]
        if o["e"] == "N":
            o["vc"] = {}
            continue
        kn = know[o["e"]]
        need = {}
        for j in o["hard"]:
            s, v = ops[j]["tick"]
            if kn.get(s, 0) < v and need.get(s, (0, 0))[0] < v:
                need[s] = (v, j)
        for s in list(need):
            if any(ops[j]["vc"].get(s, 0) >= need[s][0] for s2, (v, j) in need.items() if s2 != s):
                del need[s]
        waits[i] = [(s, v) for s, (v, j) in need.items()]
        for s, (v, j) in need.items():
            kn[s] = max(kn.get(s, 0), v)
            for s2, v2 in ops[j]["vc"].items():
                kn[s2] = max(kn.get(s2, 0), v2)
        o["vc"] = dict(kn)
    for e in "SAGVP":
        q = queue[e]
        for i in order[e]:
            o = ops[i]
            for s, v in waits[i]:
                q.wait_ge(T.sem[s], v)
            ins = o["fn"](q)
            if o["sem"] != "sent":
                ins.then_inc(T.sem[o["tick"][0]], o["inc"])
    for s in SEMAPHORES:
        g.wait_ge(T.sem[s], total[s])
